import numpy as np, ml_dtypes
CORES = [5,29,101,125,133,157,229,253]
N = 8
BF = ml_dtypes.bfloat16
W, L, ST = 4096, 256, 16
STEPS = (4, 1, 6, 3)
def look(X, J, z, w, A):
    u = np.sum(w * z, axis=2) & 1023
    h = (((J * (2 * u + 1)[:, :, None, :]) >> 5) + J + A[:, None, None, None]) & (W - 1)
    x = np.take_along_axis(X, h.reshape(N, 8, 1, 16 * L), 3).reshape(N, 8, 16, 16, L)
    m = np.minimum(x, z[:, :, :, None, :])
    return u, x, np.sum(m, axis=2), 1 + np.sum(x - m, axis=2)
def parts(rng):
    top = rng.integers(6, 16, (N, 8, 1, W))
    X = rng.integers(0, top + 1, (N, 8, 16, W)); J = rng.integers(0, W, (N, 8, 16, L))
    return X, J, rng.integers(1, 16, (N, 8, 16, L)), rng.integers(0, 64, (N, 8, 16, 1))
def pack(X, J, z, w):
    return {"xt": X.reshape(N, 128, W).astype(np.float32).astype(BF), "jn": np.ascontiguousarray(J.reshape(N, 128, L)).astype(np.int32),
            "zd": z.reshape(N, 128, L).astype(np.float32).astype(BF), "wt": w.reshape(N, 128, 1).astype(np.float32)}
def setup_inputs(rng):
    return pack(*parts(rng))
def uphill(X, J, z, w):
    u, x, g, s = look(X, J, z, w, np.zeros(N, np.int64))
    o = np.argsort(g * np.power(s.astype(np.float64), -1.0), axis=2, kind="stable")
    return np.take_along_axis(J, o, 2)
def setup_inputs_corners(rng):
    X, J, z, w = parts(rng)
    w[:, 2] = 0; w[:, 2, :4] = 63; w[:, 2, 4] = 21; J[:, 2] = rng.integers(W - 120, W, (N, 16, L))
    w[:, 3] = 63; X[:, 3, :, 0] = 15; J[:, 3, 1:8] = W - 1 - 32 * rng.integers(0, 12, (N, 7, L)); J[:, 3, 15] = 0
    J[:, :, 0, :4] = 0; J[:, :, 1, :4] = W - 1
    c = W - 1 - 32 * np.arange(12); h = ((c * 2017 >> 5) + c + 128 * L) & (W - 1)
    X[0, 3][:, h] = 1; X[0, 3][:, (h + 1) & (W - 1)] = 15
    lead = np.concatenate([J[STEPS[0], 3, 1:], J[STEPS[0], 3, :1]], axis=0)
    strong = np.zeros((N, 8, 1, L), bool); short = np.zeros((N, 8, 1, L), bool); near = np.zeros((N, 8, 1, L), bool); m = 0
    for r in range(N):
        q = r ^ STEPS[0]
        if r > q: continue
        if m == 0: strong[r] = True
        elif m == 1:
            strong[q] = True; near[q, 7, 0, L - 1] = True
        else:
            strong[r, ::2] = True; strong[q, 1::2] = True
            strong[q, 1, 0, 0] = False; strong[r, 1, 0, 0] = True; strong[r, 6, 0, L - 1] = False; strong[q, 6, 0, L - 1] = True
            if m == 3:
                short[r] = True; short[q] = True
        m += 1
    z = np.where(strong, 15, 1) + np.zeros((1, 1, 16, 1), np.int64)
    up = uphill(X, J, z, w); down = up[:, :, ::-1]; most = np.concatenate([up[:, :, 1:], up[:, :, :1]], axis=2)
    J = np.where(strong, np.where(short, down, np.where(near, most, up)), J)
    for r in range(N):
        for g in range(8): J[r, g] = np.where(strong[r, g], J[r, g], up[r, g]) if g == 3 and r != STEPS[0] else J[r, g]
    J[STEPS[0], 3] = lead
    return pack(X, J, z, w)
def setup_inputs_crowd(rng):
    X, J, z, w = parts(rng); c = rng.integers(0, W, (N, 8)); c[0, 0] = 0; c[1, 0] = W - 1
    for g in (0, 4, 1, 5):
        J[:, g] = c[:, g][:, None, None]; z[:, g] = z[:, g, :, :1].copy()
    for g, o in ((1, int(rng.integers(0, L))), (5, L - 1)):
        J[:, g, :, o] = rng.integers(0, W, (N, 16)); z[:, g, :, o] = rng.integers(1, 16, (N, 16))
    for g in (2, 6): J[:, g] = rng.choice(np.array([0, 3, W // 2, W - 1]), (N, 16, L))
    for g in (3, 7): J[:, g] = J[:, g, :1].copy()
    for a in (X, J, z, w): a[:, 4] = a[0, 4].copy()
    return pack(X, J, z, w)
def setup_inputs_ends(rng):
    X = 15 * rng.integers(0, 2, (N, 8, 16, W)); X[:, 1::2] = 15 * rng.integers(0, 2, (N, 4, 1, W))
    J = (W - 1) * rng.integers(0, 2, (N, 8, 16, L)); kind = rng.integers(0, 3, (N, 8, 1, L))
    z = np.where(kind == 0, 1, np.where(kind == 1, 15, 1 + 14 * rng.integers(0, 2, (N, 8, 16, L))))
    w = 63 * rng.integers(0, 2, (N, 8, 16, 1)); w[:, 5] = 63
    for g in (0, 3, 7): w[:, g] = 0
    c = W // 32 - 2
    X[:, 0, :, 0] = 0; X[:, 0, :, c] = 0
    X[:, 3, :, 0] = 15; X[:, 3, :, c] = 15; X[:, 3, 0, c] = 0
    J[:, 3, :, -8:] = 0; J[:, 3, 0, -8:] = W - 1; z[:, 3, :, -8:] = 15
    X[:, 7, :, 0] = 15; X[:, 7, :, c] = 15; X[:, 7, 0, c] = 0
    duo = np.array([[0, 0], [0, 1], [1, 0], [1, 1], [2, 2], [2, 3], [3, 2], [3, 3], [4, 4]])
    pn = rng.integers(0, 9, L); pn[:9] = rng.permutation(9); pn[L - 1] = 8; pn[L - 2] = 5; pn[L - 3] = 0; pn[L - 4] = 7; pn[L - 5] = 6
    for r in range(N):
        if r < (r ^ STEPS[0]): X[r, 3, 1, c] = 14
        kd = duo[pn, int(r > (r ^ STEPS[0]))]
        J[r, 7] = 0; J[r, 7, 0] = np.where(kd >= 2, W - 1, 0)
        z[r, 7] = np.where((kd == 0) | (kd == 2), 15, 1)
        z[r, 7, :7] = np.where(kd == 4, 15, z[r, 7, :7])
    return pack(X, J, z, w)
def setup_inputs_spread(rng):
    def e(*shape): return np.exp2(rng.integers(-2, 4, shape))
    X = np.minimum((16 * rng.random((N, 8, 16, W)) ** e(N, 8, 1, W)).astype(np.int64), 15)
    J = np.minimum((W * rng.random((N, 8, 16, L)) ** e(N, 8, 1, L)).astype(np.int64), W - 1)
    z = np.minimum(1 + (15 * rng.random((N, 8, 16, L)) ** e(N, 8, 1, L)).astype(np.int64), 15)
    w = np.minimum((64 * rng.random((N, 8, 16, 1)) ** e(N, 8, 16, 1)).astype(np.int64), 63)
    high = [r for r in range(N) if r > (r ^ STEPS[0])]; few = 1 + rng.permutation(3)
    for r, n in zip(high[1:], few):
        at = np.array([L - 1, 0, L // 2])[:int(n)]
        X[r, :, :, ::4] = 0; J[r] = J[r] & -128
        w[r, 7] = 0; X[r, 7, :, 1] = 15
        J[r, 7, 0][at] = 1; z[r, 7][:, at] = 15; z[r ^ STEPS[0], 7][:, at] = 1
    return pack(X, J, z, w)
def setup_inputs_ties(rng):
    X, J, z, w = parts(rng); v = rng.integers(0, 16, (8, 16)); v[:, 0] = 15; v[:, 1] = 0
    ix = (np.arange(16)[None, None, :, None] + rng.integers(0, 16, (N, 8, 1, W))) & 15
    X = np.where(rng.random((N, 8, 1, W)) < 0.0625, X, v[np.arange(8)[None, :, None, None], ix])
    one = rng.integers(1, 16, (N, 8, 1, L)); one[:, ::2] = one[0, ::2].copy(); one[:, 7] = one[0, 7].copy()
    w[:, 6] = 0; kd = rng.integers(0, 4, L); kd[:4] = rng.permutation(4); kd[L - 4:] = rng.permutation(4)
    for c, g, s, d, n in ((1, 100, 61, 8, 9), (2, 120, 57, 8, 9), (3, 110, 51, 8, 9), (4, 108, 50, 8, 9), (5, 113, 53, 8, 9), (6, 56, 131, 4, 12), (7, 60, 87, 4, 12), (8, 60, 86, 4, 12)):
        X[:, 6, :n, c] = d + (s - 1 + np.arange(n)) // n
        X[:, 6, n:, c] = (g - d * n + np.arange(16 - n)) // (16 - n)
    for m, d, p, lo, hi in ((0, 8, 1, 2, 3), (1, 8, 1, 4, 5), (2, 4, 6, 7, 8)):
        at = kd == m; one[:, 6, 0, at] = d
        for r in range(N):
            J[r, 6][:, at] = p; J[r, 6, 15, at] = hi if r > (r ^ STEPS[0]) else lo
    return pack(X, J, one + np.zeros((1, 1, 16, 1), np.int64), w)
def check_inputs(d):
    bad = []
    for k, lo, hi in (("xt", 0, 15), ("jn", 0, W - 1), ("zd", 1, 15), ("wt", 0, 63)):
        a = np.asarray(d[k]).astype(np.float64)
        if not np.all((a >= lo) & (a <= hi)): bad.append("range of " + k)
        if not np.all(a == np.floor(a)): bad.append("whole numbers of " + k)
    return bad
def reference(xt, jn, zd, wt):
    X = xt.astype(np.float32).astype(np.int64).reshape(N, 8, 16, W); J = jn.astype(np.int64).reshape(N, 8, 16, L)
    z = zd.astype(np.float32).astype(np.int64).reshape(N, 8, 16, L); w = wt.astype(np.int64).reshape(N, 8, 16, 1)
    A = np.zeros(N, np.int64); r = np.arange(N); k16 = np.arange(16)
    for step in STEPS:
        q = r ^ step
        u, x, g, s = look(X, J, z, w, A)
        G = np.add.accumulate(g, axis=2); S = np.add.accumulate(s, axis=2)
        bG, bS, b = G[:, :, 0], S[:, :, 0], np.zeros((N, 8, L), np.int64)
        for k in range(1, 16):
            up = G[:, :, k] * bS > bG * S[:, :, k]
            bG = np.where(up, G[:, :, k], bG); bS = np.where(up, S[:, :, k], bS); b = np.where(up, k, b)
        y = np.max(np.where(k16[None, None, None, :, None] <= b[:, :, None, None, :], x, 0), axis=3)
        mine = bG * bS[q]; other = bG[q] * bS
        win = (mine > other) | ((mine == other) & (r < q)[:, None, None]); ww = win[:, :, None, :]
        both = np.concatenate([J, J[q]], axis=2)
        spliced = np.take_along_axis(both, k16[None, None, :, None] + (b + 1)[:, :, None, :], 2)
        col = (ST * np.arange(L)[None, None, :] + (u & (ST - 1)))[:, :, None, :]
        old = np.take_along_axis(X, col, 3)
        np.put_along_axis(X, np.broadcast_to(col, old.shape), np.where(ww, (old + y) >> 1, old), 3)
        z = np.where(ww, np.maximum(np.abs(z - y), 1), np.maximum((z + y[q]) >> 1, 1))
        J = np.where(ww, spliced, J)
        A = np.sum(np.where(win, b + 1, 0), axis=(1, 2))
    out = X[..., :W // 2] + 16 * X[..., W // 2:]
    return {"yx": out.reshape(N, 128, W // 2).astype(np.float32).astype(BF), "yj": J.reshape(N, 128, L).astype(np.float32), "yz": z.reshape(N, 128, L).astype(np.float32).astype(BF)}

@@ -1,0 +1,603 @@
+from concourse.mybir import AluOpType as ALU, ActivationFunctionType as ACT
+
+STEPS = (4, 1, 6, 3)
+NV = 2
+JV = 2
+EARLY = 0
+PA = 2
+NE = 0
+NT = 0
+NG = 7
+LATE = 12
+LATE1 = 0
+CUT = 10
+CH = ((0, 4), (4, 8), (8, 12), (12, 16))
+C0 = 327680.0
+
+SCRATCH = {
+    "X": ("sbuf", [128, 4352], "bfloat16"),
+    "xg": ("sbuf", [128, 4096], "bfloat16"),
+    "mm": ("sbuf", [128, 4096], "bfloat16"),
+    "PM": ("sbuf", [128, 4096], "bfloat16"),
+    "Tab": ("sbuf", [128, 17 * 128], "int32"),
+    "D": ("dram", [8, 4096], "int32"),
+    "Ji": ("sbuf", [128, 256], "int32"),
+    "wc": ("sbuf", [128, 1], "float32"),
+    "BD": ("sbuf", [128, 128], "bfloat16"),
+    "BD1": ("sbuf", [128, 128], "bfloat16"),
+    "W2": ("sbuf", [128, 128], "bfloat16"),
+    "SEL": ("sbuf", [128, 144], "bfloat16"),
+    "WSEL": ("sbuf", [128, 144], "bfloat16"),
+    "ID": ("sbuf", [128, 512], "bfloat16"),
+    "CL": ("sbuf", [128, 128], "bfloat16"),
+    "C17": ("sbuf", [128, 128], "bfloat16"),
+    "BIG": ("sbuf", [128, 128], "bfloat16"),
+    "ip": ("sbuf", [128, 2], "int32"),
+    "acol": ("sbuf", [128, 2], "float32"),
+    "KT": ("sbuf", [128, 256], "float32"),
+    "iL": ("sbuf", [128, 128], "float32"),
+    "mask": ("sbuf", [128, 256], "bfloat16"),
+    "cb": ("sbuf", [128, 480], "bfloat16"),
+    "R2": ("sbuf", [128, 512], "bfloat16"),
+    "Q2": ("sbuf", [128, 512], "bfloat16"),
+    "XV": ("sbuf", [128, 512], "bfloat16"),
+    "sv": ("sbuf", [128, 256], "bfloat16"),
+    "dl": ("sbuf", [128, 384], "bfloat16"),
+    "ab": ("sbuf", [128, 256], "bfloat16"),
+    "m192": ("sbuf", [128, 256], "bfloat16"),
+    "tb": ("sbuf", [128, 256], "bfloat16"),
+    "qi": ("sbuf", [128, 256], "int32"),
+    "qj": ("sbuf", [128, 4, 64], "int32"),
+    "z3c": ("sbuf", [128, 64], "bfloat16"),
+    "Qs": ("sbuf", [128, 256], "bfloat16"),
+    "Rs": ("sbuf", [128, 256], "bfloat16"),
+    "ONE": ("sbuf", [128, 192], "bfloat16"),
+    "C6": ("sbuf", [128, 128], "bfloat16"),
+    "hh": ("sbuf", [128, 256], "uint16"),
+    "TS": ("sbuf", [128, 704], "float32"),
+    "KS": ("sbuf", [128, 480], "float32"),
+    "p2": ("sbuf", [128, 128], "float32"),
+    "sm": ("sbuf", [128, 160], "float32"),
+    "F0": ("sbuf", [128, 96], "float32"),
+    "F1": ("sbuf", [128, 96], "float32"),
+    "F2": ("sbuf", [128, 96], "float32"),
+    "si": ("sbuf", [128, 32], "int32"),
+    "wb": ("sbuf", [128, 16], "bfloat16"),
+    "ls": ("sbuf", [128, 96], "uint16"),
+    "A32": ("sbuf", [128, 1], "float32"),
+    "junk": ("sbuf", [128, 16], "float32"),
+    "YX": ("sbuf", [128, 2304], "bfloat16"),
+}
+for _t in range(5):
+    SCRATCH["J%d" % _t] = ("sbuf", [128, 256], "int32")
+    SCRATCH["z%d" % _t] = ("sbuf", [128, 256], "bfloat16")
+for _t in range(4):
+    SCRATCH["JP%d" % _t] = ("sbuf", [128, 128], "int32")
+    SCRATCH["PK%d" % _t] = ("sbuf", [128, 128], "int32")
+    SCRATCH["GT%d" % _t] = ("sbuf", [128, 64], "float32")
+    SCRATCH["GP%d" % _t] = ("sbuf", [128, 64], "float32")
+    SCRATCH["Y%d" % _t] = ("sbuf", [128, 256], "bfloat16")
+    SCRATCH["YP%d" % _t] = ("sbuf", [128, 256], "bfloat16")
+for _b in "ABCDEFGH":
+    SCRATCH["p" + _b] = ("psum", [128, 512], "float32")
+
+SEMAPHORES = ["cV", "cS", "cP", "cG", "left", "ldj", "ldz", "ldw", "ldx", "out1", "out2", "out3", "out4"]
+for _t in range(4):
+    SEMAPHORES += ["aJ%d" % _t, "aG%d" % _t, "aY%d" % _t, "dA%d" % _t, "dB%d" % _t, "tA%d" % _t, "tB%d" % _t]
+
+
+def helper(T, topo, rank):
+    me = T.cores[rank]
+    able = [c for c in topo.cores_of(me) if T.rank_of(c) is None and all(topo.may_write(c, T.cores[rank ^ s]) for s in STEPS)]
+    able.sort(key=lambda c: (topo.die(c) != topo.die(me), c))
+    return able[0]
+
+
+def route(T, topo, rank, t, kind):
+    me, to = T.cores[rank], T.cores[rank ^ STEPS[t]]
+    if topo.may_write(me, to):
+        return None, to, topo.mask(me, to)
+    via = helper(T, topo, rank)
+    return via, to, topo.mask(via, to)
+
+
+def bits(m):
+    return bin(m).count("1")
+
+
+def relay_program(g, core, T, topo):
+    left = 0
+    for rank in range(len(T.cores)):
+        for t in range(len(STEPS)):
+            for kind in "JGY":
+                via, to, m = route(T, topo, rank, t, kind)
+                if via != core:
+                    continue
+                rid, pid = topo.addr(to, core)
+                buf, sem = T["%sP%d" % (kind, t)], T.sem["a%s%d" % (kind, t)]
+                g.wait_ge(sem, bits(m))
+                g.remote_dma(buf[:], buf[:], sem, T.sem.left, pid, rid, m)
+                left += bits(m)
+    if left:
+        g.wait_ge(T.sem.left, left)
+
+
+def emit(g, T, ops, left):
+    queue = {"V": g.vector, "S": g.scalar, "P": g.tensor, "G": g, "Y": g.sync}
+    own = {"V": "cV", "S": "cS", "P": "cP", "G": "cG"}
+    last_w, readers, bank = {}, {}, {}
+    known = {q: {} for q in queue}
+    total = {}
+    for n, o in enumerate(ops):
+        if o["sem"] is not None and o["q"] is not None:
+            total[o["sem"]] = total.get(o["sem"], 0) + 16
+    used = set()
+    for n, o in enumerate(ops):
+        q = o["q"]
+        if q is None:
+            o["tok"], o["snap"] = (o["sem"], o["val"]), {}
+        else:
+            deps = set()
+            for k in o["r"]:
+                if k in last_w:
+                    deps.add(last_w[k])
+            for k in o["w"]:
+                if k in last_w:
+                    deps.add(last_w[k])
+                deps.update(readers.get(k, ()))
+            for b in o["b"]:
+                deps.update(v for qq, v in bank.get(b, {}).items() if qq != q)
+            need = {}
+            for d in deps:
+                p = ops[d]
+                if p["remote"] or (q == "P" and p["q"] == "P"):
+                    continue
+                if o["sem"] is not None and p["sem"] == o["sem"]:
+                    continue
+                s, v = p["tok"]
+                if s not in need or need[s][0] < v:
+                    need[s] = (v, d)
+            o["waits"] = []
+            for s, (v, d) in sorted(need.items(), key=lambda e: -e[1][1]):
+                if known[q].get(s, -1) >= v:
+                    continue
+                o["waits"].append(d)
+                used.add(d)
+                known[q][s] = v
+                for s2, v2 in ops[d]["snap"].items():
+                    if known[q].get(s2, -1) < v2:
+                        known[q][s2] = v2
+            o["snap"] = dict(known[q])
+            o["tok"] = (o["sem"], total[o["sem"]]) if o["sem"] is not None else (own.get(q), n)
+        for k in o["r"]:
+            readers.setdefault(k, []).append(n)
+        for k in o["w"]:
+            last_w[k] = n
+            readers[k] = []
+        for b in o["b"]:
+            bank.setdefault(b, {})[q] = n
+    count = {s: 0 for s in own.values()}
+    for n, o in enumerate(ops):
+        if o["q"] is None:
+            total[o["sem"]] = o["val"]
+            continue
+        e = queue[o["q"]]
+        for d in o["waits"]:
+            e.wait_ge(T.sem[ops[d]["tok"][0]], ops[d]["tok"][1])
+        ins = o["f"]()
+        if o["sem"] is not None:
+            ins.then_inc(T.sem[o["sem"]], 16)
+        elif n in used:
+            s = own[o["q"]]
+            count[s] += 1
+            o["tok"] = (s, count[s])
+            ins.then_inc(T.sem[s], 1)
+    total.update(count)
+    total["left"] = left
+    for s, v in total.items():
+        if v:
+            g.wait_ge(T.sem[s], v)
+
+
+def build_rank(g, core, T, topo, rank):
+    ops = []
+    left = [0]
+    V, S, P = g.vector, g.scalar, g.tensor
+
+    def op(q, f, r=(), w=(), b="", sem=None, remote=False, val=None):
+        ops.append({"q": q, "f": f, "r": list(r), "w": list(w), "b": b, "sem": sem, "remote": remote, "val": val})
+
+    def tt(out, a, b_, alu, r, w, b=""):
+        op("V", lambda: V.tensor_tensor(out, a, b_, alu), r, w, b)
+
+    def ts(out, a, s1, s2, o0, o1, r, w, b=""):
+        if s2 is None:
+            op("V", lambda: V.tensor_scalar(out, a, s1, None, o0), r, w, b)
+        else:
+            op("V", lambda: V.tensor_scalar(out, a, s1, s2, o0, o1), r, w, b)
+
+    def cp(out, a, r, w, b=""):
+        op("V", lambda: V.tensor_copy(out, a), r, w, b)
+
+    def scan(out, d0, d1, o0, o1, r, w, b=""):
+        op("V", lambda: V.tensor_tensor_scan(out, d0, d1, 0.0, o0, o1), r, w, b)
+
+    def fill(ap, v, w):
+        op("V", lambda: V.memset(ap, v), (), w)
+
+    def act(out, a, fn, r, w, b="", **kw):
+        op("S", lambda: S.activation(out, a, fn, **kw), r, w, b)
+
+    def mat(out, lhsT, rhs, start, stop, r, w, b):
+        op("P", lambda: P.matmul(out, lhsT, rhs, start, stop), r, w, b)
+
+    def dma(q, out, a, sem, r, w):
+        e = g.sync if q == "Y" else S
+        op(q, lambda: e.dma_start(out, a), r, w, sem=sem)
+
+    def send(t, kind, src, r):
+        via, to, m = route(T, topo, rank, t, kind)
+        rid, pid = topo.addr(to if via is None else via, core)
+        dst, sem = "%sP%d" % (kind, t), "a%s%d" % (kind, t)
+        left[0] += bits(m)
+        op("G", lambda: g.remote_dma(T[dst][:], T[src][:], T.sem[sem], T.sem.left, pid, rid, m), r, (), remote=True)
+        op(None, None, (), [dst], sem=sem, val=bits(route(T, topo, rank ^ STEPS[t], t, kind)[2]))
+
+    def weave(fn, quarters):
+        got = []
+        for q in quarters:
+            n = len(ops)
+            fn(q)
+            got.append(ops[n:])
+            del ops[n:]
+        for step in zip(*got):
+            ops.extend(step)
+
+    IDN, HALF, NEG2, SIXT = (T.ID[:, 128 * j:128 * j + 128] for j in range(4))
+    lsY, lsC, lsW, lsJ, lsX = (T.ls[:, 16 * j:16 * j + 16] for j in range(5))
+    kb0, i16, dmp, dmp3, dmp3x = (T.iL[:, 16 * j:16 * j + 16] for j in range(3, 8))
+    C0K = ["C0_%d" % q for q in range(4)]
+
+    dma("Y", T.sv[:], T.zd[:], "ldz", (), ["sva", "svb"])
+    dma("S", T.wc[:], T.wt[:], "ldw", (), ["wc"])
+    dma("Y", T.Ji[:], T.jn[:], "ldj", (), ["Ji"])
+    dma("Y", T.X[:, 0:4096], T.xt[:], "ldx", (), ["X"])
+    fill(T.ONE[:], 1.0, ["ones"])
+    op("G", lambda: g.affine_select(T.BD1[:], T.ONE[:, 0:128], [[-16, 8], [0, 16]], ALU.is_ge, 0.0, 0, 1), ["ones"], ["BD1"])
+    op("G", lambda: g.affine_select(T.BD[:], T.BD1[:], [[16, 8], [0, 16]], ALU.is_ge, 0.0, 15, -1), ["BD1"], ["BD"])
+    op("G", lambda: g.iota(T.ip[:, 0:1], [[0, 1]], 0, 1), (), ["ip0"])
+    op("G", lambda: g.iota(T.iL[:, 0:16], [[16, 16]], 0, 0, allow_small_or_imprecise_dtypes=True), (), ["iL0"])
+    op("G", lambda: g.affine_select(IDN, T.ONE[:, 0:128], [[-1, 128]], ALU.is_equal, 0.0, 0, 1), ["ones"], ["IDN"])
+    op("G", lambda: g.iota(T.KT[:], [[1024, 4], [16, 4], [1, 16]], 0, 0, allow_small_or_imprecise_dtypes=True), (), ["KT"])
+    fill(T.CL[0:32, :], C0 / 32, ["CL0"])
+    fill(T.CL[32:64, :], 33.0 / 32, ["CL1"])
+    fill(T.A32[:], 0.0, ["A32"])
+    fill(T.SEL[:], 0.0, ["SEL"])
+    fill(T.WSEL[:], 0.0, ["WSEL"])
+    fill(T.C17[0:32, :], 2.0 ** -17, ["C17"])
+    fill(T.mask[:], 1.0, ["mask"])
+    fill(T.cb[:], 1.0, ["cb0", "cb1", "cb2", "cb3"])
+    fill(T.BIG[:], 2.0 ** 17, ["BIG"])
+    fill(T.Q2[:, 256:512], -64.0, ["Q2c"])
+    fill(T.m192[:], -192.0, ["m192"])
+    fill(T.R2[:, 0:256], 193.0, ["R2c"])
+    fill(T.C6[0:32, :], 6.0, ["C6"])
+    fill(T.mask[:, 0:256:16], 0.0, ["mask"])
+    ts(T.SEL[:, 15:143:16], T.BD[:, 0:128:16], 2.0 ** -12, None, ALU.mult, None, ["BD"], ["SEL"])
+    ts(T.ip[:, 1:2], T.ip[:, 0:1], 15, None, ALU.bitwise_and, None, ["ip0"], ["ip1"])
+    cp(T.acol[:, 0:1], T.ip[:, 1:2], ["ip1"], ["ac0"])
+    ts(T.acol[:, 1:2], T.ip[:, 1:2], 64.0, None, ALU.mult, None, ["ip1"], ["ac1"])
+    fill(T.F0[:], 0.0, ["F0c", "Dl", "b256"])
+    for dst, key, mul in ((T.F1[:, 1:32:2], "F1c", 1.0), (i16, "i16", 16.0)):
+        ts(dst, T.iL[:, 0:16], T.acol[:, 0:1], mul, ALU.add, ALU.mult, ["iL0", "ac0"], [key])
+    for at in (33, 49):
+        ts(T.F1[:, at:at + 15:2], T.iL[:, 0:8], T.acol[:, 0:1], None, ALU.add, None, ["iL0", "ac0"], ["F1c"])
+    ts(T.F1[:, 65:96:2], T.iL[:, 0:16], T.acol[:, 0:1], 4096.0, ALU.add, ALU.add, ["iL0", "ac0"], ["F1x"])
+    fill(T.F0[:, 1:32:2], 256.0, ["F0c"])
+    for dst, key, add in ((dmp, "dmp", 4096.0), (dmp3, "dmp3", 2048.0), (T.iL[:, 112:120], "dmp3x", 2048.0)):
+        n = 16 if key != "dmp3x" else 8
+        ts(dst, T.iL[:, 0:n], T.acol[:, 0:1], add, ALU.add, ALU.add, ["iL0", "ac0"], [key])
+    ts(T.iL[:, 120:128], T.iL[:, 8:16], T.acol[:, 0:1], 4096.0, ALU.add, ALU.add, ["iL0", "ac0"], ["dmp3y"])
+
+    PARTS = ((range(0, PA), T.pA, "A"), (range(PA, 4), T.pB, "B"))
+
+    def u_start():
+        for qs, U, b in PARTS:
+            n = 64 * len(qs)
+            mat(U[:, 0:n], T.CL[0:64, :], T.ONE[0:64, 0:n], True, False, ["CL0", "CL1", "ones"], ["U" + b], b)
+            mat(U[:, 0:n], T.W2[:], T.m192[:, 0:n], False, False, ["W2", "m192"], ["U" + b], b)
+        mat(T.pD[:, 0:256], IDN, T.m192[:], True, False, ["IDN", "m192"], ["zP"], "D")
+
+    ts(T.W2[:], T.BD[:], T.wc[:, 0:1], 2.0, ALU.mult, ALU.mult, ["BD", "wc"], ["W2"])
+    ts(T.z0[:], T.sv[:], 192.0, None, ALU.add, None, ["sva"], ["z0_%d" % q for q in range(4)])
+    u_start()
+    ts(T.WSEL[:, 15:143:16], T.BD[:, 0:128:16], T.wc[:, 0:1], None, ALU.mult, None, ["BD", "wc"], ["WSEL"])
+    cp(T.J0[:, 0:128], T.Ji[:, 0:128], ["Ji"], ["J0A"])
+    ts(T.J0[:, 128:256], T.Ji[:, 128:256], 4096.0, None, ALU.mult, None, ["Ji"], ["J0B"])
+
+    def late_constants():
+        ts(HALF, IDN, 0.5, None, ALU.mult, None, ["IDN"], ["HALF"])
+        ts(NEG2, IDN, -2.0, None, ALU.mult, None, ["IDN"], ["NEG2"])
+        ts(SIXT, IDN, 16.0, None, ALU.mult, None, ["IDN"], ["SIXT"])
+        ts(T.KT[:], T.KT[:], T.acol[:, 1:2], 2.0 ** -12, ALU.add, ALU.mult, ["KT", "ac1"], ["KT"])
+        ts(kb0, T.KT[:, 0:256:16], -2.0 ** -12, None, ALU.add, None, ["KT"], ["kb0"])
+
+    def names_out(t):
+        J = "PK%d" % t
+        tt(T[J][:], T["J%d" % t][:, 0:128], T["J%d" % t][:, 128:256], ALU.add, ["J%dA" % t, "J%dB" % t], [J])
+        send(t, "J", J, [J])
+        dma("Y", T.D[:, 0:2048], T[J][:], "dA%d" % t, [J], ["Da"])
+        for k in range(16):
+            dma("Y", T.Tab[k:128:16, 0:(16 - k) * 128], T.D[:, k * 128:2048], "tA%d" % t, ["Da"], ["TabA"])
+        dma("Y", T.D[:, 2048:4096], T["JP%d" % t][:], "dB%d" % t, ["JP%d" % t], ["Db"])
+        rival_part(t, range(16 - (LATE1 if route(T, topo, rank, t, "Y")[0] is None else LATE)), [])
+
+    def rival_part(t, ks, after):
+        for k in ks:
+            dma("Y", T.Tab[k:128:16, (16 - k) * 128:17 * 128], T.D[:, 2048:2048 + (k + 1) * 128], "tB%d" % t, ["Db"] + after, ["TabB"])
+
+    def picks(t, part):
+        qs, U, b = part
+        z, J, base = T["z%d" % t], T["J%d" % t], 64 * qs[0]
+        mat(U[:, 0:64 * len(qs)], T.W2[:], z[:, base:base + 64 * len(qs)], False, True,
+            ["W2"] + ["z%d_%d" % (t, q) for q in qs], ["U" + b], b)
+
+        def chain(q):
+            lo, hi, p = 64 * q, 64 * q + 64, str(q)
+            u = U[:, lo - base:hi - base]
+            ts(T.tb[:, lo:hi], u, -1056.0, None, ALU.add, None, ["U" + b], ["tb" + p], b)
+            tt(T.pC[:, lo:hi], u, T.tb[:, lo:hi], ALU.subtract, ["U" + b, "tb" + p], [C0K[q]], b + "C")
+            tt(T.pC[:, lo:hi], T.pC[:, lo:hi], J[:, lo:hi], ALU.mult, [C0K[q], "J%d%s" % (t, b)], [C0K[q]], "C")
+            ts(T.qi[:, lo:hi], T.pC[:, lo:hi], 1.0 if b == "A" else 2.0 ** -12, T.A32[:, 0:1], ALU.mult, ALU.add,
+               [C0K[q], "A32"], ["qi" + p], "C")
+            ts(T.qj[:, q, :], T.qi[:, lo:hi], 5, 4095, ALU.arith_shift_right, ALU.bitwise_and, ["qi" + p], ["qj" + p])
+        weave(chain, qs)
+        for r in range(4):
+            cp(T.hh[:, base + r:base + 64 * len(qs):4], T.qj[:, qs[0]:qs[-1] + 1, 16 * r:16 * r + 16], ["qj%d" % q for q in qs],
+               ["hh%s%d" % (b, r)])
+
+    def hk(j):
+        return ["hh%s%d" % ("A" if j < PA else "B", r) for r in range(4)]
+
+    def splice(t, h):
+        ts(T["J%d" % (t + 1)][:, 128 * h:128 * h + 128], T.Tab[:, 0:17 * 128].indirect(T.ls[:, 48 + 8 * h:56 + 8 * h]),
+           4095 << (12 * h), None, ALU.bitwise_and, None, ["TabA", "TabB", "lsJ"], ["J%d%s" % (t + 1, "AB"[h])])
+
+    def choose(h):
+        lo, hi, off = 128 * h, 128 * h + 128, T.ls[:, 32 + 8 * h:40 + 8 * h]
+        act(T.Qs[:, lo:hi], T.Q2[:, 0:512].indirect(off), ACT.Copy, ["Q2", "Q2c", "lsW"], ["Qs%d" % h])
+        act(T.Rs[:, lo:hi], T.R2[:, 0:512].indirect(off), ACT.Copy, ["R2c", "zW", "lsW"], ["Rs%d" % h])
+
+    def demand(t, h):
+        lo, hi, b = 128 * h, 128 * h + 128, "EF"[h]
+        mat(T["p" + b][:, 0:128], IDN, T.Qs[:, lo:hi], False, False, ["IDN", "Qs%d" % h], ["pz" + b], b)
+        mat(T["p" + b][:, 0:128], IDN, T["YP%d" % t][:, lo:hi], False, True, ["IDN", "YP%d" % t], ["pz" + b], b)
+        tt(T["z%d" % (t + 1)][:, lo:hi], T["p" + b][:, 0:128], T.Rs[:, lo:hi], ALU.max, ["pz" + b, "Rs%d" % h],
+           ["z%d_%d" % (t + 1, 2 * h), "z%d_%d" % (t + 1, 2 * h + 1)], b)
+
+    def units(name, c0, c1):
+        return ["%s%d" % (name, c) for c in range(c0, c1)]
+
+    names_out(0)
+    picks(0, PARTS[0])
+    for t in range(4):
+        lower = rank < (rank ^ STEPS[t])
+        zt, zk = T["z%d" % t], ["z%d_%d" % (t, q) for q in range(4)]
+        GT, GP, Y = T["GT%d" % t], T["GP%d" % t], T["Y%d" % t]
+        todo = list(range(16))
+
+        def max_scan(n):
+            for c in todo[:n]:
+                scan(T.PM[:, 256 * c:256 * c + 256], T.mask[:], T.xg[:, 256 * c:256 * c + 256], ALU.mult, ALU.max, ["mask", "xg%d" % c], ["PM%d" % c])
+            del todo[:n]
+
+        def pick_s(j):
+            c0, c1 = CH[j][0], CH[j][1] - (NV if j == JV else 0)
+            for c0, c1 in ((c0, c1),) if j < 3 else ((c0, c0 + 2), (c0 + 2, c1)):
+                act(T.xg[:, 256 * c0:256 * c1], T.X[:, 0:4096].indirect(T.hh[:, 16 * c0:16 * c1]), ACT.Copy, ["X"] + hk(j), units("xg", c0, c1))
+        for j in PARTS[0][0]:
+            pick_s(j)
+        picks(t, PARTS[1])
+        if t == 0:
+            late_constants()
+        zoff = 192.0
+        for j in range(16):
+            at = 64 * (j // 4) + j % 4
+            mat(T.pD[:, at:at + 61:4], IDN, zt[:, 16 * j:16 * j + 16], False, j == 15, ["IDN"] + zk, ["zP"], "D")
+        for a in range(16):
+            mat(T.pG[:, 256:272], T.WSEL[:, 15 - a:143 - a], zt[:, a:256:16], a == 0, a == 15, ["WSEL"] + zk, ["uL", "pe"], "G")
+        for tb_, b in ((T.pF, "F"), (T.pH, "H")):
+            mat(tb_[:, 0:128], T.C17[0:32, :], T.ONE[0:32, 0:128], True, False, ["C17", "ones"], ["Tp" + b], b)
+
+        gpos, tpos = (0, 32) if lower else (32, 0)
+        Gs = [(T.pC, 256, 1), (T.pC, 1, 2), (T.pC, 257, 2), (T.pC, 1, 2)]
+        Go = [(T.pC, 0), (T.pC, 256), (T.pC, 0), (GT, gpos)]
+        Ts = [(T.TS, 0, 1), (T.TS, 257, 2), (T.TS, 513, 2), (T.TS, 641, 2)]
+        To = [(T.TS, 256), (T.TS, 512), (T.TS, 640), (GT, tpos)]
+        Ks = [(T.KT, 0, 1), (T.KS, 1, 2), (T.KS, 257, 2), (T.KS, 385, 2)]
+        Ko = [(T.KS, 0), (T.KS, 256), (T.KS, 384), (T.KS, 448)]
+        cpos = (0, 256, 384, 448)
+
+        def prefix_t(h):
+            b = "FH"[h]
+            scan(T.TS[:, 128 * h:128 * h + 128], T.mask[:, 0:128], T["p" + b][:, 0:128], ALU.mult, ALU.add, ["mask", "Tp" + b], ["TS0_%d" % h], b)
+
+        def prefix_g(h):
+            b = "EG"[h]
+            scan(T.pC[:, 256 + 128 * h:384 + 128 * h], T.mask[:, 0:128], T["p" + b][:, 0:128], ALU.mult, ALU.add,
+                 ["mask", "Gp" + b], ["C1_%d" % h], b + "C")
+
+        def level(lv, h, f1, f2):
+            m, at = (128, 128 * h) if lv == 0 else (256 >> lv, 0)
+
+            def view(src, first, step):
+                lo = src[1] + at * src[2]
+                return src[0][:, lo + first * src[2]:lo + (m - 1) * src[2] + 1:src[2] * step]
+
+            def out(dst):
+                return dst[0][:, dst[1] + at:dst[1] + at + m]
+            gk = (["C1_%d" % h], C0K, ["C1_0"], C0K)[lv]
+            gw = (C0K[2 * h:2 * h + 2], ["C1_0"], C0K, ["GTg%d" % t])[lv]
+            tk = (["TS0_%d" % h], ["TS1_0", "TS1_1"], ["TS2_0"], ["TS3_0"])[lv]
+            kk = (["KT"], ["KS1_0", "KS1_1"], ["KS2_0"], ["KS3_0"])[lv]
+            ck = "cb%d" % lv
+            c = T.cb[:, cpos[lv] + at:cpos[lv] + at + m]
+            tt(T.pA[:, 256:256 + m // 2], view(Gs[lv], 1, 2), view(Ts[lv], 0, 2), ALU.mult, gk + tk, ["p1", "zxA"], "AC")
+            tt(T.p2[:, 0:m // 2], view(Gs[lv], 0, 2), view(Ts[lv], 1, 2), ALU.mult, gk + tk, ["p2"], "C")
+            max_scan(f1)
+            tt(T.cb[:, cpos[lv] + at + 1:cpos[lv] + at + m:2], T.pA[:, 256:256 + m // 2], T.p2[:, 0:m // 2], ALU.is_gt,
+               ["p1", "p2"], [ck], "A")
+            max_scan(f2)
+            scan(out(Go[lv]), c, view(Gs[lv], 0, 1), ALU.add, ALU.min, [ck] + gk, gw, "C")
+            scan(out(To[lv]), c, view(Ts[lv], 0, 1), ALU.add, ALU.min, [ck] + tk, ["TS%d_%d" % (lv + 1, h) if lv < 3 else "GTt%d" % t])
+            if lv == 3:
+                send(t, "G", "GT%d" % t, ["GTg%d" % t, "GTt%d" % t])
+            scan(out(Ko[lv]), c, view(Ks[lv], 0, 1), ALU.add, ALU.min, [ck] + kk, ["KS%d_%d" % (lv + 1, h)])
+
+        for j in PARTS[1][0]:
+            pick_s(j)
+        cp(T.z3c[:], T.pD[:, 192:256], ["zP"], ["z3c"], "D")
+        if NV:
+            c0, c1 = CH[JV][1] - NV, CH[JV][1]
+            cp(T.xg[:, 256 * c0:256 * c1], T.X[:, 0:4096].indirect(T.hh[:, 16 * c0:16 * c1]), ["X"] + hk(JV), units("xg", c0, c1))
+        for j, (c0, c1) in enumerate(CH):
+            bt, bg, at = "FH"[j // 2], "EG"[j // 2], 64 * (j % 2)
+            lo, hi = 256 * c0, 256 * c1
+            if j == 3:
+                for h, b in enumerate("AB"):
+                    xk = units("xg", c0 + 2 * h, c0 + 2 * h + 2)
+                    for a in range(8 * h, 8 * h + 8):
+                        mat(T["p" + bt][:, at:at + 64], T.SEL[:, 15 - a:143 - a], T.xg[:, lo + 64 * a:lo + 64 * a + 64], False,
+                            a == 15, ["SEL"] + xk, ["Tp" + bt], bt)
+                    tt(T.mm[:, lo + 512 * h:lo + 512 * h + 512], T.xg[:, lo + 512 * h:lo + 512 * h + 512], T["p" + b][:, 0:512], ALU.min,
+                       ["zx" + b] + xk, ["mm3_%d" % h], b)
+                    for a in range(8 * h, 8 * h + 8):
+                        mat(T["p" + bg][:, at:at + 64], T.SEL[:, 15 - a:143 - a], T.mm[:, lo + 64 * a:lo + 64 * a + 64], a == 0, a == 15,
+                            ["SEL", "mm3_%d" % h], ["Gp" + bg], bg)
+                continue
+            for a in range(16):
+                mat(T["p" + bt][:, at:at + 64], T.SEL[:, 15 - a:143 - a], T.xg[:, lo + 64 * a:lo + 64 * a + 64], False,
+                    j % 2 == 1 and a == 15, ["SEL"] + units("xg", c0, c1), ["Tp" + bt], bt)
+            if j == 0:
+                for h, b in enumerate("AB"):
+                    for k in range(16):
+                        mat(T["p" + b][:, k:512:16], IDN, T.z3c[:, 32 * h:32 * h + 32], True, True, ["IDN", "z3c"],
+                            ["zx" + b, "U" + b, "o" + b], b)
+            for k in range(16):
+                tt(T.mm[:, lo + k:hi:16], T.xg[:, lo + k:hi:16], T.pD[:, 16 * c0:16 * c1], ALU.min,
+                   ["zP"] + units("xg", c0, c1), ["mm%d_%d" % (j, k)], "D")
+            for a in range(16):
+                mat(T["p" + bg][:, at:at + 64], T.SEL[:, 15 - a:143 - a], T.mm[:, lo + 64 * a:lo + 64 * a + 64], a == 0, a == 15,
+                    ["SEL"] + ["mm%d_%d" % (j, k) for k in range(16)], ["Gp" + bg], bg)
+            if j == 0:
+                cp(T.si[:, 0:16], T.pG[:, 256:272], ["uL"], ["si0"], "G")
+            if j == 1:
+                ts(T.si[:, 16:32], T.si[:, 0:16], 15, None, ALU.bitwise_and, None, ["si0"], ["si1"])
+                max_scan(NE)
+            if j == 2:
+                prefix_g(0)
+                prefix_t(0)
+                tt(T.sm[:, 0:16], T.si[:, 16:32], i16, ALU.add, ["si1", "i16"], ["sm0"])
+                if EARLY:
+                    level(0, 0, 1, 1)
+                cp(lsC, T.sm[:, 0:16], ["sm0"], ["lsC"])
+        if not EARLY:
+            level(0, 0, 1, 1)
+        prefix_t(1)
+        max_scan(NT)
+        act(T.XV[:, 0:256], T.X[:, 0:4096].indirect(lsC), ACT.Identity, ["X", "lsC"], ["XVo"], bias=192.0)
+        act(T.Q2[:, 0:256], zt[:], ACT.Identity, zk, ["Q2"], bias=-0.25 - zoff / 2, scale=0.5)
+        if t == 3:
+            for j, (bank, b) in enumerate(((T.pB, "B"), (T.pE, "E"), (T.pF, "F"), (T.pB, "B"))):
+                col = 512 * j
+                mat(bank[:, 0:512], IDN, T.X[:, col:col + 512], True, False, ["IDN", "X"], ["o" + b], b)
+                mat(bank[:, 0:512], SIXT, T.X[:, 2048 + col:2048 + col + 512], False, True, ["SIXT", "X"], ["o" + b], b)
+                act(T.YX[:, col:col + 512], bank[:, 0:512], ACT.Copy, ["o" + b], ["YX"], b)
+        prefix_g(1)
+        tt(T.F0[:, 65:96:2], T.sm[:, 0:16], dmp if t < 3 else dmp3x, ALU.subtract, ["sm0", "dmp", "dmp3x", "dmp3y"], ["Dl"])
+        for lv in range(4):
+            ng = NG if route(T, topo, rank, t, "Y")[0] is None else 8
+            level(lv, 1 if lv == 0 else 0, 1 if 7 - 2 * lv <= ng else 0, 1 if 8 - 2 * lv <= ng else 0)
+        Kb = T.KS[:, 449:480:2]
+        if t < 3:
+            u_start()
+        max_scan(1)
+        ts(lsY, Kb, 4096.0, None, ALU.mult, None, ["KS4_0"], ["lsY"])
+        if route(T, topo, rank, t, "Y")[0] is None:
+            rival_part(t, range(16 - LATE1, 16), ["lsY"])
+        max_scan(max(0, len(todo) - 4))
+        act(Y[:, 0:192], T.PM[:, 0:3072].indirect(T.ls[:, 0:12]), ACT.Copy, units("PM", 0, 12) + ["lsY"], ["Ya%d" % t], scale=0.5)
+        max_scan(4)
+        tt(T.sm[:, 16:32], Kb, kb0, ALU.subtract, ["KS4_0", "kb0"], ["b1"])
+        ts(Y[:, 192:256], T.PM[:, 0:4096].indirect(T.ls[:, 12:16]), 0.5, None, ALU.mult, None, units("PM", 0, 16) + ["lsY"], ["Yb%d" % t])
+        yk = ["Ya%d" % t, "Yb%d" % t]
+        send(t, "Y", "Y%d" % t, yk)
+        ts(T.F0[:, 33:64:2], T.sm[:, 16:32], 2.0 ** 19, None, ALU.mult, None, ["b1", "F0c"], ["b256"])
+        if t == 3:
+            cp(T.F1[:, 65:96:2], dmp3, ["dmp3"], ["F1x"])
+        mat(T.pG[:, 256:512], HALF, T.XV[:, 0:256], True, False, ["HALF", "XVo"], ["pe", "oG"], "G")
+        mat(T.pG[:, 256:512], IDN, Y[:], False, True, ["IDN"] + yk, ["pe"], "G")
+        mat(T.pH[:, 256:512], IDN, zt[:], True, False, ["IDN"] + zk, ["pd", "oH"], "H")
+        mat(T.pH[:, 256:512], NEG2, Y[:], False, True, ["NEG2"] + yk, ["pd"], "H")
+        act(T.XV[:, 256:512], T.pG[:, 256:512], ACT.Identity, ["pe"], ["XVn"], "G", bias=95.75)
+        if route(T, topo, rank, t, "Y")[0] is not None:
+            rival_part(t, range(16 - LATE, 16), ["XVn"])
+        act(T.ab[:], T.pH[:, 256:512], ACT.Abs, ["pd"], ["ab"], "H", bias=-zoff)
+        for b in "EF":
+            mat(T["p" + b][:, 0:128], T.C6[0:32, :], T.ONE[0:32, 0:128], True, False, ["C6", "ones"], ["pz" + b], b)
+        if t == 3:
+            ts(T.ls[:, 80:88], T.sm[:, 8:16], -2048.0, None, ALU.add, None, ["sm0"], ["lsH"])
+            tt(T.dl[:, 0:256], T.XV[:, 256:512], T.XV[:, 0:256], ALU.subtract, ["XVo", "XVn"], ["dl"])
+        ts(T.R2[:, 256:512], T.ab[:], 1.0, 192.0, ALU.max, ALU.add, ["ab"], ["zW"])
+        if t == 3:
+            tt(T.sv[:, 0:128], T.YX[:, 0:2048].indirect(T.ls[:, 16:24]), T.dl[:, 0:128], ALU.add, ["YX", "lsC", "dl"], ["sva"])
+            ts(T.dl[:, 256:384], T.dl[:, 128:256], 16.0, None, ALU.mult, None, ["dl"], ["dl16"])
+        tt(T.sm[:, 32:64], GT[:, 1:64:2], GP[:, 1:64:2], ALU.mult, ["GTg%d" % t, "GTt%d" % t, "GP%d" % t], ["pr"])
+        for j in range(3):
+            win = T.F1[:, 32 * j:32 * j + 32:2]
+            if lower:
+                tt(win, T.sm[:, 32:48], T.sm[:, 48:64], ALU.is_ge, ["pr"], ["win%d" % j])
+            else:
+                tt(win, T.sm[:, 48:64], T.sm[:, 32:48], ALU.is_gt, ["pr"], ["win%d" % j])
+        scan(T.F2[:], T.F0[:], T.F1[:], ALU.mult, ALU.add, ["win0", "win1", "win2", "F0c", "F1c", "F1x", "Dl", "b256"], ["F2"])
+        if t < 3:
+            tt(T.wb[:], T.F1[:, 0:32:2], T.sm[:, 16:32], ALU.mult, ["win0", "b1"], ["wb"])
+        cp(T.ls[:, 32:80], T.F2[:, 1:96:2], ["F2"], ["lsW", "lsJ", "lsX"])
+        choose(0)
+        if t < 3:
+            splice(t, 0)
+            tt(T.X[:, 0:4352].indirect(T.ls[:, 64:64 + CUT]), T.XV[:, 256:256 + 16 * CUT], T.m192[:, 0:16 * CUT], ALU.add,
+               ["XVn", "m192", "lsX"], ["X"])
+            mat(T.pG[:, 0:16], T.BIG[:], T.wb[:], True, True, ["BIG", "wb"], ["pa"], "G")
+            act(T.junk[:], T.pG[:, 0:16], ACT.Copy, ["pa"], ["junk", "A32"], "G", accum_out=T.A32[:, 0:1])
+        choose(1)
+        if t < 3:
+            demand(t, 0)
+            tt(T.X[:, 0:4352].indirect(T.ls[:, 64 + CUT:80]), T.XV[:, 256 + 16 * CUT:512], T.m192[:, 16 * CUT:256], ALU.add,
+               ["XVn", "m192", "lsX"], ["X"])
+            picks(t + 1, PARTS[0])
+            demand(t, 1)
+            splice(t, 1)
+            names_out(t + 1)
+    cp(T.YX[:, 0:2304].indirect(T.ls[:, 64:72]), T.sv[:, 0:128], ["sva", "lsX"], ["YX"])
+    tt(T.sv[:, 128:256], T.YX[:, 0:2048].indirect(T.ls[:, 80:88]), T.dl[:, 256:384], ALU.add, ["YX", "lsH", "dl16"], ["svb"])
+    cp(T.YX[:, 0:2304].indirect(T.ls[:, 72:80]), T.sv[:, 128:256], ["svb", "lsX"], ["YX"])
+    dma("Y", T.yx[:], T.YX[:, 0:2048], "out2", ["YX"], ())
+    splice(3, 0)
+    demand(3, 0)
+    demand(3, 1)
+    splice(3, 1)
+    act(T.tb[:], T.z4[:], ACT.Identity, ["z4_%d" % q for q in range(4)], ["tb%d" % q for q in range(4)], bias=-192.0)
+    dma("S", T.yz[:], T.tb[:], "out4", ["tb0"], ())
+    cp(T.KS[:, 0:128], T.J4[:, 0:128], ["J4A"], ["KS1_0"])
+    ts(T.KS[:, 128:256], T.J4[:, 128:256], 2.0 ** -12, None, ALU.mult, None, ["J4B"], ["KS1_1"])
+    dma("Y", T.yj[:], T.KS[:, 0:256], "out1", ["KS1_0", "KS1_1"], ())
+    emit(g, T, ops, left[0])
+
+
+def rank_program(g, core, T, topo):
+    rank = T.rank_of(core)
+    if rank is None:
+        relay_program(g, core, T, topo)
+    else:
+        build_rank(g, core, T, topo, rank)

@@ -1,34 +1,54 @@
+import numpy as np
 from concourse.mybir import AluOpType as ALU, ActivationFunctionType as ACT
 
 STEPS = (4, 1, 6, 3)
-NV = 2
-JV = 2
-EARLY = 0
-PA = 2
-NE = 0
-NT = 0
-NG = 7
-LATE = 12
-LATE1 = 0
-CUT = 10
-CH = ((0, 4), (4, 8), (8, 12), (12, 16))
+PAR = {
+    "NV": (3, 2, 2, 2),
+    "S1": (2, 1, 0),
+    "G1": (0, 0, 0),
+    "H0": 8,
+    "JE": (2, 2, 2),
+    "JM": (0, 0, 0),
+    "PK": (0, 0, 0),
+    "LB": 5,
+    "ZW": 7,
+    "CA": 0,
+    "ORD": ((0, 0), (0, 1), (0, 2), (1, 0), (0, 3), (1, 1), (1, 2), (1, 3)),
+    "VC": (0, 1, 1, 1),
+    "N2": (0, 0, 0, 0),
+    "J2": 1,
+    "NT": 0,
+    "NG": 8,
+    "YS": 12,
+    "CUT": 16,
+    "YSPLIT": (0, 0, 0, 0),
+    "DB": (0, 15),
+    "JW": (0, 0, 0, 0),
+    "QW": (1, 1, 1, 0),
+    "GN": 16,
+    "LATE": (0, 0),
+}
+CH = ((0, 4), (4, 8), (8, 14), (14, 16))
+NA = 64
 C0 = 327680.0
+LOW = 0.375
 
 SCRATCH = {
     "X": ("sbuf", [128, 4352], "bfloat16"),
     "xg": ("sbuf", [128, 4096], "bfloat16"),
     "mm": ("sbuf", [128, 4096], "bfloat16"),
+    "zq": ("sbuf", [128, 64], "bfloat16"),
     "PM": ("sbuf", [128, 4096], "bfloat16"),
-    "Tab": ("sbuf", [128, 17 * 128], "int32"),
+    "Tab": ("sbuf", [128, 2048], "int32"),
     "D": ("dram", [8, 4096], "int32"),
     "Ji": ("sbuf", [128, 256], "int32"),
     "wc": ("sbuf", [128, 1], "float32"),
     "BD": ("sbuf", [128, 128], "bfloat16"),
     "BD1": ("sbuf", [128, 128], "bfloat16"),
-    "W2": ("sbuf", [128, 128], "bfloat16"),
+    "W2": ("sbuf", [128, 256], "bfloat16"),
     "SEL": ("sbuf", [128, 144], "bfloat16"),
     "WSEL": ("sbuf", [128, 144], "bfloat16"),
-    "ID": ("sbuf", [128, 512], "bfloat16"),
+    "ID": ("sbuf", [128, 768], "bfloat16"),
     "CL": ("sbuf", [128, 128], "bfloat16"),
     "C17": ("sbuf", [128, 128], "bfloat16"),
     "BIG": ("sbuf", [128, 128], "bfloat16"),
@@ -36,42 +56,47 @@ SCRATCH = {
     "acol": ("sbuf", [128, 2], "float32"),
     "KT": ("sbuf", [128, 256], "float32"),
     "iL": ("sbuf", [128, 128], "float32"),
-    "mask": ("sbuf", [128, 256], "bfloat16"),
+    "mask": ("sbuf", [128, 192], "bfloat16"),
+    "mk": ("sbuf", [128, 256], "bfloat16"),
     "cb": ("sbuf", [128, 480], "bfloat16"),
-    "R2": ("sbuf", [128, 512], "bfloat16"),
-    "Q2": ("sbuf", [128, 512], "bfloat16"),
+    "Z2": ("sbuf", [128, 512], "bfloat16"),
+    "Q2": ("sbuf", [128, 512], "float32"),
     "XV": ("sbuf", [128, 512], "bfloat16"),
     "sv": ("sbuf", [128, 256], "bfloat16"),
     "dl": ("sbuf", [128, 384], "bfloat16"),
     "ab": ("sbuf", [128, 256], "bfloat16"),
+    "zr": ("sbuf", [128, 256], "bfloat16"),
     "m192": ("sbuf", [128, 256], "bfloat16"),
+    "m192h": ("sbuf", [128, 256], "bfloat16"),
     "tb": ("sbuf", [128, 256], "bfloat16"),
+    "tw": ("sbuf", [128, 256], "bfloat16"),
     "qi": ("sbuf", [128, 256], "int32"),
     "qj": ("sbuf", [128, 4, 64], "int32"),
-    "z3c": ("sbuf", [128, 64], "bfloat16"),
-    "Qs": ("sbuf", [128, 256], "bfloat16"),
-    "Rs": ("sbuf", [128, 256], "bfloat16"),
+    "Jw": ("sbuf", [128, 256], "int32"),
+    "Jo": ("sbuf", [128, 256], "float32"),
     "ONE": ("sbuf", [128, 192], "bfloat16"),
-    "C6": ("sbuf", [128, 128], "bfloat16"),
+    "ONEh": ("sbuf", [128, 256], "bfloat16"),
     "hh": ("sbuf", [128, 256], "uint16"),
     "TS": ("sbuf", [128, 704], "float32"),
     "KS": ("sbuf", [128, 480], "float32"),
     "p2": ("sbuf", [128, 128], "float32"),
-    "sm": ("sbuf", [128, 160], "float32"),
-    "F0": ("sbuf", [128, 96], "float32"),
-    "F1": ("sbuf", [128, 96], "float32"),
-    "F2": ("sbuf", [128, 96], "float32"),
+    "sm": ("sbuf", [128, 96], "float32"),
+    "b1": ("sbuf", [128, 16], "float32"),
+    "F0": ("sbuf", [128, 64], "float32"),
+    "F1": ("sbuf", [128, 64], "float32"),
+    "F2": ("sbuf", [128, 64], "float32"),
     "si": ("sbuf", [128, 32], "int32"),
     "wb": ("sbuf", [128, 16], "bfloat16"),
     "ls": ("sbuf", [128, 96], "uint16"),
     "A32": ("sbuf", [128, 1], "float32"),
+    "ub": ("sbuf", [128, 1], "float32"),
     "junk": ("sbuf", [128, 16], "float32"),
     "YX": ("sbuf", [128, 2304], "bfloat16"),
 }
 for _t in range(5):
-    SCRATCH["J%d" % _t] = ("sbuf", [128, 256], "int32")
     SCRATCH["z%d" % _t] = ("sbuf", [128, 256], "bfloat16")
 for _t in range(4):
+    SCRATCH["JJ%d" % _t] = ("sbuf", [128, 512], "float32")
     SCRATCH["JP%d" % _t] = ("sbuf", [128, 128], "int32")
     SCRATCH["PK%d" % _t] = ("sbuf", [128, 128], "int32")
     SCRATCH["GT%d" % _t] = ("sbuf", [128, 64], "float32")
@@ -83,7 +108,7 @@ for _b in "ABCDEFGH":
 
 SEMAPHORES = ["cV", "cS", "cP", "cG", "left", "ldj", "ldz", "ldw", "ldx", "out1", "out2", "out3", "out4"]
 for _t in range(4):
-    SEMAPHORES += ["aJ%d" % _t, "aG%d" % _t, "aY%d" % _t, "dA%d" % _t, "dB%d" % _t, "tA%d" % _t, "tB%d" % _t]
+    SEMAPHORES += ["aJ%d" % _t, "aG%d" % _t, "aY%d" % _t, "aZ%d" % _t, "dA%d" % _t, "dB%d" % _t, "tA%d" % _t, "tB%d" % _t]
 
 
 def helper(T, topo, rank):
@@ -93,30 +118,39 @@ def helper(T, topo, rank):
     return able[0]
 
 
-def route(T, topo, rank, t, kind):
+def route(T, topo, rank, t):
     me, to = T.cores[rank], T.cores[rank ^ STEPS[t]]
     if topo.may_write(me, to):
-        return None, to, topo.mask(me, to)
+        return None, to, topo.mask(me, to), topo.mask(me, to)
     via = helper(T, topo, rank)
-    return via, to, topo.mask(via, to)
+    return via, to, topo.mask(me, via), topo.mask(via, to)
 
 
 def bits(m):
     return bin(m).count("1")
 
 
+def split(t):
+    return PAR["YSPLIT"][t]
+
+
+def letters(t):
+    ys = [("Y", "Y", 0, NA), ("Z", "Y", NA, 256)] if split(t) else [("Y", "Y", 0, 256)]
+    return [("J", "J", 0, 128), ("G", "G", 0, 64)] + ys
+
+
 def relay_program(g, core, T, topo):
     left = 0
     for rank in range(len(T.cores)):
         for t in range(len(STEPS)):
-            for kind in "JGY":
-                via, to, m = route(T, topo, rank, t, kind)
-                if via != core:
-                    continue
-                rid, pid = topo.addr(to, core)
-                buf, sem = T["%sP%d" % (kind, t)], T.sem["a%s%d" % (kind, t)]
-                g.wait_ge(sem, bits(m))
-                g.remote_dma(buf[:], buf[:], sem, T.sem.left, pid, rid, m)
+            via, to, m0, m = route(T, topo, rank, t)
+            if via != core:
+                continue
+            rid, pid = topo.addr(to, core)
+            for kind, name, lo, hi in letters(t):
+                buf, sem = T["%sP%d" % (name, t)][:, lo:hi], T.sem["a%s%d" % (kind, t)]
+                g.wait_ge(sem, bits(m0))
+                g.remote_dma(buf, buf, sem, T.sem.left, pid, rid, m)
                 left += bits(m)
     if left:
         g.wait_ge(T.sem.left, left)
@@ -125,28 +159,31 @@ def relay_program(g, core, T, topo):
 def emit(g, T, ops, left):
     queue = {"V": g.vector, "S": g.scalar, "P": g.tensor, "G": g, "Y": g.sync}
     own = {"V": "cV", "S": "cS", "P": "cP", "G": "cG"}
-    last_w, readers, bank = {}, {}, {}
+    last_w, last_r, bank = {}, {}, {}
     known = {q: {} for q in queue}
     total = {}
-    for n, o in enumerate(ops):
+    for o in ops:
         if o["sem"] is not None and o["q"] is not None:
             total[o["sem"]] = total.get(o["sem"], 0) + 16
     used = set()
     for n, o in enumerate(ops):
         q = o["q"]
+        for name, size, at in o["r"] + o["w"]:
+            if name not in last_w:
+                last_w[name], last_r[name] = np.full(size, -1), {}
+        banks = {name for name, size, at in o["r"] + o["w"] if name in SCRATCH and SCRATCH[name][0] == "psum"}
         if q is None:
             o["tok"], o["snap"] = (o["sem"], o["val"]), {}
         else:
             deps = set()
-            for k in o["r"]:
-                if k in last_w:
-                    deps.add(last_w[k])
-            for k in o["w"]:
-                if k in last_w:
-                    deps.add(last_w[k])
-                deps.update(readers.get(k, ()))
-            for b in o["b"]:
+            for name, size, at in o["r"] + o["w"]:
+                deps.update(np.unique(last_w[name][at]).tolist())
+            for name, size, at in o["w"]:
+                for seen in last_r[name].values():
+                    deps.add(int(seen[at].max()))
+            for b in banks:
                 deps.update(v for qq, v in bank.get(b, {}).items() if qq != q)
+            deps.discard(-1)
             need = {}
             for d in deps:
                 p = ops[d]
@@ -169,12 +206,11 @@ def emit(g, T, ops, left):
                         known[q][s2] = v2
             o["snap"] = dict(known[q])
             o["tok"] = (o["sem"], total[o["sem"]]) if o["sem"] is not None else (own.get(q), n)
-        for k in o["r"]:
-            readers.setdefault(k, []).append(n)
-        for k in o["w"]:
-            last_w[k] = n
-            readers[k] = []
-        for b in o["b"]:
+        for name, size, at in o["r"]:
+            last_r[name].setdefault(o["sem"] or q, np.full(size, -1))[at] = n
+        for name, size, at in o["w"]:
+            last_w[name][at] = n
+        for b in banks:
             bank.setdefault(b, {})[q] = n
     count = {s: 0 for s in own.values()}
     for n, o in enumerate(ops):
@@ -203,395 +239,538 @@ def build_rank(g, core, T, topo, rank):
     ops = []
     left = [0]
     V, S, P = g.vector, g.scalar, g.tensor
+    grid = {}
 
-    def op(q, f, r=(), w=(), b="", sem=None, remote=False, val=None):
-        ops.append({"q": q, "f": f, "r": list(r), "w": list(w), "b": b, "sem": sem, "remote": remote, "val": val})
+    def A(name, *idx, rows=slice(None), key=None):
+        ap = T[name][(rows,) + idx] if idx else T[name][rows]
+        if key:
+            return ap, [(key, 1, np.zeros(1, int))]
+        if name not in grid:
+            shape = list(T[name].shape)[1:]
+            grid[name] = np.arange(int(np.prod(shape))).reshape(shape)
+        return ap, [(name, grid[name].size, grid[name][idx].reshape(-1))]
 
-    def tt(out, a, b_, alu, r, w, b=""):
-        op("V", lambda: V.tensor_tensor(out, a, b_, alu), r, w, b)
+    def C(name, lo, hi, step=1, rows=slice(None)):
+        return A(name, slice(lo, hi, step) if step > 1 else slice(lo, hi), rows=rows)
 
-    def ts(out, a, s1, s2, o0, o1, r, w, b=""):
-        if s2 is None:
-            op("V", lambda: V.tensor_scalar(out, a, s1, None, o0), r, w, b)
+    def pick(win, off, more=()):
+        return win[0].indirect(off[0]), win[1] + off[1] + list(more), off[1]
+
+    def op(q, f, r=(), w=(), sem=None, remote=False, val=None):
+        rd = [e for a in r if isinstance(a, tuple) for e in a[1]] + [e for a in w if len(a) == 3 for e in a[2]]
+        wr = [e for a in w for e in (a[1] if len(a) == 2 else a[1][:1])]
+        ops.append({"q": q, "f": f, "r": rd, "w": wr, "sem": sem, "remote": remote, "val": val})
+
+    def num(x):
+        return x[0] if isinstance(x, tuple) else x
+
+    def tt(out, a, b, alu):
+        op("V", lambda: V.tensor_tensor(out[0], a[0], b[0], alu), [a, b], [out])
+
+    def ts(out, a, s1, o0, s2=None, o1=None):
+        if o1 is None:
+            op("V", lambda: V.tensor_scalar(out[0], a[0], num(s1), None, o0), [a, s1], [out])
         else:
-            op("V", lambda: V.tensor_scalar(out, a, s1, s2, o0, o1), r, w, b)
+            op("V", lambda: V.tensor_scalar(out[0], a[0], num(s1), num(s2), o0, o1), [a, s1, s2], [out])
 
-    def cp(out, a, r, w, b=""):
-        op("V", lambda: V.tensor_copy(out, a), r, w, b)
+    def cp(out, a):
+        op("V", lambda: V.tensor_copy(out[0], a[0]), [a], [out])
 
-    def scan(out, d0, d1, o0, o1, r, w, b=""):
-        op("V", lambda: V.tensor_tensor_scan(out, d0, d1, 0.0, o0, o1), r, w, b)
+    def scan(out, d0, d1, o0, o1, first=0.0):
+        op("V", lambda: V.tensor_tensor_scan(out[0], d0[0], d1[0], first, o0, o1), [d0, d1], [out])
 
-    def fill(ap, v, w):
-        op("V", lambda: V.memset(ap, v), (), w)
+    def fill(out, v):
+        op("V", lambda: V.memset(out[0], v), (), [out])
 
-    def act(out, a, fn, r, w, b="", **kw):
-        op("S", lambda: S.activation(out, a, fn, **kw), r, w, b)
+    def act(out, a, fn=ACT.Identity, bias=None, scale=None, acc=None):
+        kw = {}
+        if bias is not None:
+            kw["bias"] = num(bias)
+        if scale is not None:
+            kw["scale"] = scale
+        if acc is not None:
+            kw["accum_out"] = acc[0]
+        op("S", lambda: S.activation(out[0], a[0], fn if bias is not None or fn != ACT.Identity else ACT.Copy, **kw), [a, bias], [out] + ([acc] if acc else []))
 
-    def mat(out, lhsT, rhs, start, stop, r, w, b):
-        op("P", lambda: P.matmul(out, lhsT, rhs, start, stop), r, w, b)
+    def mat(out, lhsT, rhs, start, stop):
+        op("P", lambda: P.matmul(out[0], lhsT[0], rhs[0], start, stop), [lhsT, rhs], [out])
 
-    def dma(q, out, a, sem, r, w):
+    def dma(q, out, a, sem, after=()):
         e = g.sync if q == "Y" else S
-        op(q, lambda: e.dma_start(out, a), r, w, sem=sem)
+        op(q, lambda: e.dma_start(out[0], a[0]), [a] + list(after), [out], sem=sem)
 
-    def send(t, kind, src, r):
-        via, to, m = route(T, topo, rank, t, kind)
+    def send(t, kind, src):
+        via, to, m, _ = route(T, topo, rank, t)
         rid, pid = topo.addr(to if via is None else via, core)
-        dst, sem = "%sP%d" % (kind, t), "a%s%d" % (kind, t)
+        name, lo, hi = [e[1:] for e in letters(t) if e[0] == kind][0]
+        dst, sem = "%sP%d" % (name, t), "a%s%d" % (kind, t)
         left[0] += bits(m)
-        op("G", lambda: g.remote_dma(T[dst][:], T[src][:], T.sem[sem], T.sem.left, pid, rid, m), r, (), remote=True)
-        op(None, None, (), [dst], sem=sem, val=bits(route(T, topo, rank ^ STEPS[t], t, kind)[2]))
+        op("G", lambda: g.remote_dma(T[dst][:, lo:hi], T[src][:, lo:hi], T.sem[sem], T.sem.left, pid, rid, m), [C(src, lo, hi)], (), remote=True)
+        op(None, None, (), [C(dst, lo, hi)], sem=sem, val=bits(route(T, topo, rank ^ STEPS[t], t)[3]))
 
-    def weave(fn, quarters):
+    def weave(*chains):
         got = []
-        for q in quarters:
+        for fn in chains:
             n = len(ops)
-            fn(q)
+            fn()
             got.append(ops[n:])
             del ops[n:]
-        for step in zip(*got):
-            ops.extend(step)
+        for k in range(max(len(c) for c in got)):
+            ops.extend(c[k] for c in got if k < len(c))
 
-    IDN, HALF, NEG2, SIXT = (T.ID[:, 128 * j:128 * j + 128] for j in range(4))
-    lsY, lsC, lsW, lsJ, lsX = (T.ls[:, 16 * j:16 * j + 16] for j in range(5))
-    kb0, i16, dmp, dmp3, dmp3x = (T.iL[:, 16 * j:16 * j + 16] for j in range(3, 8))
-    C0K = ["C0_%d" % q for q in range(4)]
+    IDN, HALF, NEG2, SIXT, NEG, NEGH = (C("ID", 128 * j, 128 * j + 128) for j in range(6))
+    W2, W2H = C("W2", 0, 128), C("W2", 128, 256)
+    lsY, lsC, lsW, lsX, lsJ = (C("ls", 16 * j, 16 * j + 16) for j in range(5))
+    lane, kb0, cj, i16, dmp, dmp3, dmp3x = (C("iL", 16 * j, 16 * j + 16) for j in range(1, 8))
+    a0 = C("acol", 0, 1)
+    A32 = A("A32")
+    K32, K64 = slice(0, 32), slice(0, 64)
+    PARTS = ((0, NA, 0, NA), (NA, 256, 2 * NA, 256 + NA))
 
-    dma("Y", T.sv[:], T.zd[:], "ldz", (), ["sva", "svb"])
-    dma("S", T.wc[:], T.wt[:], "ldw", (), ["wc"])
-    dma("Y", T.Ji[:], T.jn[:], "ldj", (), ["Ji"])
-    dma("Y", T.X[:, 0:4096], T.xt[:], "ldx", (), ["X"])
-    fill(T.ONE[:], 1.0, ["ones"])
-    op("G", lambda: g.affine_select(T.BD1[:], T.ONE[:, 0:128], [[-16, 8], [0, 16]], ALU.is_ge, 0.0, 0, 1), ["ones"], ["BD1"])
-    op("G", lambda: g.affine_select(T.BD[:], T.BD1[:], [[16, 8], [0, 16]], ALU.is_ge, 0.0, 15, -1), ["BD1"], ["BD"])
-    op("G", lambda: g.iota(T.ip[:, 0:1], [[0, 1]], 0, 1), (), ["ip0"])
-    op("G", lambda: g.iota(T.iL[:, 0:16], [[16, 16]], 0, 0, allow_small_or_imprecise_dtypes=True), (), ["iL0"])
-    op("G", lambda: g.affine_select(IDN, T.ONE[:, 0:128], [[-1, 128]], ALU.is_equal, 0.0, 0, 1), ["ones"], ["IDN"])
-    op("G", lambda: g.iota(T.KT[:], [[1024, 4], [16, 4], [1, 16]], 0, 0, allow_small_or_imprecise_dtypes=True), (), ["KT"])
-    fill(T.CL[0:32, :], C0 / 32, ["CL0"])
-    fill(T.CL[32:64, :], 33.0 / 32, ["CL1"])
-    fill(T.A32[:], 0.0, ["A32"])
-    fill(T.SEL[:], 0.0, ["SEL"])
-    fill(T.WSEL[:], 0.0, ["WSEL"])
-    fill(T.C17[0:32, :], 2.0 ** -17, ["C17"])
-    fill(T.mask[:], 1.0, ["mask"])
-    fill(T.cb[:], 1.0, ["cb0", "cb1", "cb2", "cb3"])
-    fill(T.BIG[:], 2.0 ** 17, ["BIG"])
-    fill(T.Q2[:, 256:512], -64.0, ["Q2c"])
-    fill(T.m192[:], -192.0, ["m192"])
-    fill(T.R2[:, 0:256], 193.0, ["R2c"])
-    fill(T.C6[0:32, :], 6.0, ["C6"])
-    fill(T.mask[:, 0:256:16], 0.0, ["mask"])
-    ts(T.SEL[:, 15:143:16], T.BD[:, 0:128:16], 2.0 ** -12, None, ALU.mult, None, ["BD"], ["SEL"])
-    ts(T.ip[:, 1:2], T.ip[:, 0:1], 15, None, ALU.bitwise_and, None, ["ip0"], ["ip1"])
-    cp(T.acol[:, 0:1], T.ip[:, 1:2], ["ip1"], ["ac0"])
-    ts(T.acol[:, 1:2], T.ip[:, 1:2], 64.0, None, ALU.mult, None, ["ip1"], ["ac1"])
-    fill(T.F0[:], 0.0, ["F0c", "Dl", "b256"])
-    for dst, key, mul in ((T.F1[:, 1:32:2], "F1c", 1.0), (i16, "i16", 16.0)):
-        ts(dst, T.iL[:, 0:16], T.acol[:, 0:1], mul, ALU.add, ALU.mult, ["iL0", "ac0"], [key])
-    for at in (33, 49):
-        ts(T.F1[:, at:at + 15:2], T.iL[:, 0:8], T.acol[:, 0:1], None, ALU.add, None, ["iL0", "ac0"], ["F1c"])
-    ts(T.F1[:, 65:96:2], T.iL[:, 0:16], T.acol[:, 0:1], 4096.0, ALU.add, ALU.add, ["iL0", "ac0"], ["F1x"])
-    fill(T.F0[:, 1:32:2], 256.0, ["F0c"])
-    for dst, key, add in ((dmp, "dmp", 4096.0), (dmp3, "dmp3", 2048.0), (T.iL[:, 112:120], "dmp3x", 2048.0)):
-        n = 16 if key != "dmp3x" else 8
-        ts(dst, T.iL[:, 0:n], T.acol[:, 0:1], add, ALU.add, ALU.add, ["iL0", "ac0"], [key])
-    ts(T.iL[:, 120:128], T.iL[:, 8:16], T.acol[:, 0:1], 4096.0, ALU.add, ALU.add, ["iL0", "ac0"], ["dmp3y"])
+    dma("Y", A("z0"), A("zd"), "ldz")
+    dma("S", A("wc"), A("wt"), "ldw")
+    dma("Y", A("Ji"), A("jn"), "ldj")
+    dma("Y", C("X", 0, 4096), A("xt"), "ldx")
+    fill(A("ONE"), 1.0)
+    op("G", lambda: g.affine_select(T.BD1[:], T.ONE[:, 0:128], [[-16, 8], [0, 16]], ALU.is_ge, 0.0, 0, 1), [A("ONE")], [A("BD1")])
+    op("G", lambda: g.affine_select(T.BD[:], T.BD1[:], [[16, 8], [0, 16]], ALU.is_ge, 0.0, 15, -1), [A("BD1")], [A("BD")])
+    op("G", lambda: g.affine_select(IDN[0], T.ONE[:, 0:128], [[-1, 128]], ALU.is_equal, 0.0, 0, 1), [A("ONE")], [IDN])
+    op("G", lambda: g.iota(T.ip[:, 0:1], [[0, 1]], 0, 1), (), [C("ip", 0, 1)])
+    op("G", lambda: g.iota(T.iL[:, 0:16], [[16, 16]], 0, 0, allow_small_or_imprecise_dtypes=True), (), [C("iL", 0, 16)])
+    op("G", lambda: g.iota(T.KT[:], [[1024, 4], [16, 4], [1, 16]], 0, 0, allow_small_or_imprecise_dtypes=True), (), [A("KT")])
+    fill(A("CL", rows=K32, key="CL0"), C0 / 32)
+    fill(A("CL", rows=slice(32, 64), key="CL1"), 33.0 / 32)
+    CL = (T.CL[0:64, :], A("CL", key="CL0")[1] + A("CL", key="CL1")[1])
+    fill(C("ONEh", 0, 128), 1.0)
+    fill(C("ONEh", 128, 256), 2.0 ** -12)
+    fill(A("SEL"), 0.0)
+    fill(A("WSEL"), 0.0)
+    fill(A("C17", rows=K32), 2.0 ** -17)
+    fill(A("mask"), 1.0)
+    fill(A("mk"), 99.0)
+    fill(A("cb"), 1.0)
+    fill(A("BIG"), 2.0 ** 17)
+    fill(A("m192"), -192.0)
+    fill(C("m192h", 0, 128), -192.0)
+    fill(C("m192h", 128, 256), -192.0 * 2.0 ** -12)
+    fill(A("F0"), 0.0)
+    fill(C("mask", 0, 192, 16), 0.0)
+    fill(C("mk", 0, 256, 16), LOW)
+    fill(C("F0", 1, NA // 8, 2), float(NA))
+    fill(C("F0", NA // 8 + 1, 32, 2), 256.0 - NA)
+    ts(W2, A("BD"), A("wc"), ALU.mult, 2.0, ALU.mult)
+    ts(W2H, A("BD"), A("wc"), ALU.mult, 2.0 ** -11, ALU.mult)
+    ts(NEG, IDN, -1.0, ALU.mult)
+    ts(NEGH, IDN, -2.0 ** -12, ALU.mult)
 
-    PARTS = ((range(0, PA), T.pA, "A"), (range(PA, 4), T.pB, "B"))
+    def u_start(bank, lo, hi, shifted):
+        mat(C(bank, lo, hi), CL, C("ONEh", lo, hi, rows=K64), True, False)
+        if shifted:
+            mat(C(bank, lo, hi), W2, C("m192h", lo, hi), False, False)
 
-    def u_start():
-        for qs, U, b in PARTS:
-            n = 64 * len(qs)
-            mat(U[:, 0:n], T.CL[0:64, :], T.ONE[0:64, 0:n], True, False, ["CL0", "CL1", "ones"], ["U" + b], b)
-            mat(U[:, 0:n], T.W2[:], T.m192[:, 0:n], False, False, ["W2", "m192"], ["U" + b], b)
-        mat(T.pD[:, 0:256], IDN, T.m192[:], True, False, ["IDN", "m192"], ["zP"], "D")
+    def halves(lo, hi):
+        return [(a, b) for a, b in ((lo, min(hi, 128)), (max(lo, 128), hi)) if a < b]
 
-    ts(T.W2[:], T.BD[:], T.wc[:, 0:1], 2.0, ALU.mult, ALU.mult, ["BD", "wc"], ["W2"])
-    ts(T.z0[:], T.sv[:], 192.0, None, ALU.add, None, ["sva"], ["z0_%d" % q for q in range(4)])
-    u_start()
-    ts(T.WSEL[:, 15:143:16], T.BD[:, 0:128:16], T.wc[:, 0:1], None, ALU.mult, None, ["BD", "wc"], ["WSEL"])
-    cp(T.J0[:, 0:128], T.Ji[:, 0:128], ["Ji"], ["J0A"])
-    ts(T.J0[:, 128:256], T.Ji[:, 128:256], 4096.0, None, ALU.mult, None, ["Ji"], ["J0B"])
+    def u_sum(bank, lo, hi, z, at):
+        for a, b in halves(lo, hi):
+            mat(C(bank, a, b), W2 if a < 128 else W2H, C(z, at + a - lo, at + b - lo), False, False)
 
-    def late_constants():
-        ts(HALF, IDN, 0.5, None, ALU.mult, None, ["IDN"], ["HALF"])
-        ts(NEG2, IDN, -2.0, None, ALU.mult, None, ["IDN"], ["NEG2"])
-        ts(SIXT, IDN, 16.0, None, ALU.mult, None, ["IDN"], ["SIXT"])
-        ts(T.KT[:], T.KT[:], T.acol[:, 1:2], 2.0 ** -12, ALU.add, ALU.mult, ["KT", "ac1"], ["KT"])
-        ts(kb0, T.KT[:, 0:256:16], -2.0 ** -12, None, ALU.add, None, ["KT"], ["kb0"])
+    def u_cast(bank, lo, hi, tb, shifted):
+        act(C(tb, lo, hi), C(bank, lo, hi), bias=A("ub") if shifted else C0 + 33 - 1056)
+
+    def u_rest(bank, lo, hi, tb):
+        for a, b in halves(lo, hi):
+            mat(C(bank, a, b), NEG if a < 128 else NEGH, C(tb, a, b), False, b == hi)
+
+    def names_pack(t):
+        J = "JJ%d" % t
+        for lo, at in ((0, 0), (NA, 2 * NA)):
+            n = NA if lo == 0 else 128 - NA
+            tt(C("PK%d" % t, lo, lo + n), C(J, at, at + n), C(J, 128 + NA + lo, 128 + NA + lo + n), ALU.add)
 
     def names_out(t):
-        J = "PK%d" % t
-        tt(T[J][:], T["J%d" % t][:, 0:128], T["J%d" % t][:, 128:256], ALU.add, ["J%dA" % t, "J%dB" % t], [J])
-        send(t, "J", J, [J])
-        dma("Y", T.D[:, 0:2048], T[J][:], "dA%d" % t, [J], ["Da"])
+        send(t, "J", "PK%d" % t)
+        dma("Y", C("D", 0, 2048), A("PK%d" % t), "dA%d" % t)
         for k in range(16):
-            dma("Y", T.Tab[k:128:16, 0:(16 - k) * 128], T.D[:, k * 128:2048], "tA%d" % t, ["Da"], ["TabA"])
-        dma("Y", T.D[:, 2048:4096], T["JP%d" % t][:], "dB%d" % t, ["JP%d" % t], ["Db"])
-        rival_part(t, range(16 - (LATE1 if route(T, topo, rank, t, "Y")[0] is None else LATE)), [])
+            if k == (PAR["DB"][far(t)]):
+                dma("Y", C("D", 2048, 4096), A("JP%d" % t), "dB%d" % t)
+            if k < 15:
+                dma("Y", A("Tab", slice(0, (15 - k) * 128), rows=slice(k, 128, 16), key="TabA"), C("D", (k + 1) * 128, 2048), "tA%d" % t)
+        rival_part(t, range(16 - late(t)), [])
+
+    def far(t):
+        return int(route(T, topo, rank, t)[0] is not None)
+
+    def late(t):
+        return PAR["LATE"][far(t)]
 
     def rival_part(t, ks, after):
         for k in ks:
-            dma("Y", T.Tab[k:128:16, (16 - k) * 128:17 * 128], T.D[:, 2048:2048 + (k + 1) * 128], "tB%d" % t, ["Db"] + after, ["TabB"])
+            dma("Y", A("Tab", slice((15 - k) * 128, 2048), rows=slice(k, 128, 16), key="TabB"), C("D", 2048, 2048 + (k + 1) * 128), "tB%d" % t, after)
 
-    def picks(t, part):
-        qs, U, b = part
-        z, J, base = T["z%d" % t], T["J%d" % t], 64 * qs[0]
-        mat(U[:, 0:64 * len(qs)], T.W2[:], z[:, base:base + 64 * len(qs)], False, True,
-            ["W2"] + ["z%d_%d" % (t, q) for q in qs], ["U" + b], b)
+    def both_lists(t, old):
+        got = []
+        for part in range(2):
+            n = len(ops)
+            lists(t, part, old)
+            got.append(ops[n:])
+            del ops[n:]
+        for n, (part, k) in enumerate(PAR["ORD"]):
+            if t and n == PAR["PK"][old]:
+                names_pack(t)
+                names_out(t)
+            ops.extend(got[part][k:k + 1] if k < 3 else got[part][3:])
+        c1 = 4 * PAR["VC"][t] + 4
+        c0 = c1 - PAR["NV"][t]
+        if c0 < c1:
+            cp(C("xg", 256 * c0, 256 * c1), records(c0, c1))
 
-        def chain(q):
-            lo, hi, p = 64 * q, 64 * q + 64, str(q)
-            u = U[:, lo - base:hi - base]
-            ts(T.tb[:, lo:hi], u, -1056.0, None, ALU.add, None, ["U" + b], ["tb" + p], b)
-            tt(T.pC[:, lo:hi], u, T.tb[:, lo:hi], ALU.subtract, ["U" + b, "tb" + p], [C0K[q]], b + "C")
-            tt(T.pC[:, lo:hi], T.pC[:, lo:hi], J[:, lo:hi], ALU.mult, [C0K[q], "J%d%s" % (t, b)], [C0K[q]], "C")
-            ts(T.qi[:, lo:hi], T.pC[:, lo:hi], 1.0 if b == "A" else 2.0 ** -12, T.A32[:, 0:1], ALU.mult, ALU.add,
-               [C0K[q], "A32"], ["qi" + p], "C")
-            ts(T.qj[:, q, :], T.qi[:, lo:hi], 5, 4095, ALU.arith_shift_right, ALU.bitwise_and, ["qi" + p], ["qj" + p])
-        weave(chain, qs)
+    def records(c0, c1):
+        return pick(C("X", 0, 4096), C("hh", 16 * c0, 16 * c1))
+
+    def lists(t, part, old):
+        lo, hi, at, _ = PARTS[part]
+        tt(C("Q2", at, at + hi - lo), C("pD" if part == 0 else "pE", lo, hi), C("JJ%d" % old, at, at + hi - lo), ALU.mult)
+        if t == 0:
+            cp(C("qi", lo, hi), C("Q2", at, at + hi - lo))
+        else:
+            ts(C("qi", lo, hi), pick(C("Q2", 0, 2 * hi), C("ls", 32 + lo // 16, 32 + hi // 16)), A32, ALU.add)
+        js = slice(lo // 64, hi // 64)
+        ts(A("qj", js), C("qi", lo, hi), 5, ALU.arith_shift_right, 4095, ALU.bitwise_and)
         for r in range(4):
-            cp(T.hh[:, base + r:base + 64 * len(qs):4], T.qj[:, qs[0]:qs[-1] + 1, 16 * r:16 * r + 16], ["qj%d" % q for q in qs],
-               ["hh%s%d" % (b, r)])
+            cp(C("hh", lo + r, hi, 4), A("qj", js, slice(16 * r, 16 * r + 16)))
 
-    def hk(j):
-        return ["hh%s%d" % ("A" if j < PA else "B", r) for r in range(4)]
+    def factors(z, ats, parts):
+        for part in parts:
+            (lo, hi, _, _), at, side = PARTS[part], ats[part], ("pF", "pA")[part]
+            mat(C(side, lo, hi), W2, C(z, at, at + hi - lo), True, True)
+            u_sum(("pD", "pE")[part], lo, hi, z, at)
+            u_cast(side, lo, hi, "tb", z == "Z2")
+            if PAR["CA"]:
+                u_rest(("pD", "pE")[part], PARTS[part][0], PARTS[part][1], "tb")
+        for part in parts if not PAR["CA"] else ():
+            u_rest(("pD", "pE")[part], PARTS[part][0], PARTS[part][1], "tb")
 
-    def splice(t, h):
-        ts(T["J%d" % (t + 1)][:, 128 * h:128 * h + 128], T.Tab[:, 0:17 * 128].indirect(T.ls[:, 48 + 8 * h:56 + 8 * h]),
-           4095 << (12 * h), None, ALU.bitwise_and, None, ["TabA", "TabB", "lsJ"], ["J%d%s" % (t + 1, "AB"[h])])
+    def yx(h, spare=0):
+        return C("YX", 1152 * h, 1152 * h + 1024 + spare)
 
-    def choose(h):
-        lo, hi, off = 128 * h, 128 * h + 128, T.ls[:, 32 + 8 * h:40 + 8 * h]
-        act(T.Qs[:, lo:hi], T.Q2[:, 0:512].indirect(off), ACT.Copy, ["Q2", "Q2c", "lsW"], ["Qs%d" % h])
-        act(T.Rs[:, lo:hi], T.R2[:, 0:512].indirect(off), ACT.Copy, ["R2c", "zW", "lsW"], ["Rs%d" % h])
-
-    def demand(t, h):
-        lo, hi, b = 128 * h, 128 * h + 128, "EF"[h]
-        mat(T["p" + b][:, 0:128], IDN, T.Qs[:, lo:hi], False, False, ["IDN", "Qs%d" % h], ["pz" + b], b)
-        mat(T["p" + b][:, 0:128], IDN, T["YP%d" % t][:, lo:hi], False, True, ["IDN", "YP%d" % t], ["pz" + b], b)
-        tt(T["z%d" % (t + 1)][:, lo:hi], T["p" + b][:, 0:128], T.Rs[:, lo:hi], ALU.max, ["pz" + b, "Rs%d" % h],
-           ["z%d_%d" % (t + 1, 2 * h), "z%d_%d" % (t + 1, 2 * h + 1)], b)
-
-    def units(name, c0, c1):
-        return ["%s%d" % (name, c) for c in range(c0, c1)]
-
+    u_start("pD", 0, NA, False)
+    u_start("pE", NA, 256, False)
+    factors("z0", (0, NA), (0, 1))
+    mat(C("pC", 0, 1), CL, C("ONEh", 0, 1, rows=K64), True, False)
+    mat(C("pC", 0, 1), W2, C("m192h", 0, 1), False, True)
+    act(A("ub"), C("pC", 0, 1), bias=-1056.0)
+    ts(C("SEL", 15, 143, 16), C("BD", 0, 128, 16), 2.0 ** -12, ALU.mult)
+    ts(C("WSEL", 15, 143, 16), C("BD", 0, 128, 16), A("wc"), ALU.mult)
+    ts(C("ip", 1, 2), C("ip", 0, 1), 15, ALU.bitwise_and)
+    ts(HALF, IDN, 0.5, ALU.mult)
+    cp(a0, C("ip", 1, 2))
+    ts(C("acol", 1, 2), C("ip", 1, 2), 64.0, ALU.mult)
+    ts(NEG2, IDN, -2.0, ALU.mult)
+    ts(lane, C("iL", 0, 16), a0, ALU.add)
+    ts(A("KT"), A("KT"), C("acol", 1, 2), ALU.add, 2.0 ** -12, ALU.mult)
+    ts(SIXT, IDN, 16.0, ALU.mult)
+    cp(C("JJ0", 0, NA), C("Ji", 0, NA))
+    cp(C("JJ0", 2 * NA, 128 + NA), C("Ji", NA, 128))
+    ts(C("JJ0", 128 + NA, 256 + NA), C("Ji", 128, 256), 4096.0, ALU.mult)
+    ts(i16, lane, 16.0, ALU.mult)
+    names_pack(0)
     names_out(0)
-    picks(0, PARTS[0])
+    ts(C("F1", 1, NA // 8, 2), C("iL", 16, 16 + NA // 16), 0.0, ALU.add)
+    ts(C("F1", NA // 8 + 1, 32, 2), C("iL", 16 + NA // 16, 32), float(NA), ALU.add)
+    ts(C("F1", 33, 64, 2), lane, 4096.0, ALU.add)
+    ts(dmp, lane, 4096.0, ALU.add)
+    for j in range(4):
+        ts(C("iL", 96 + 4 * j, 100 + 4 * j), C("iL", 16, 20), 1024.0, ALU.add)
+        ts(C("iL", 112 + 4 * j, 116 + 4 * j), C("iL", 16, 20), 1024.0 * (j + 1), ALU.add)
+    ts(kb0, C("KT", 0, 256, 16), -2.0 ** -12, ALU.add)
+    ts(C("sm", 0, 8), C("iL", 16, 24), 2.0 ** -19, ALU.mult)
+    ts(C("sm", 8, 16), C("iL", 24, 32), 2.0 ** -19, ALU.mult, -2.0 ** -12, ALU.add)
+    tt(cj, C("sm", 0, 16), C("KT", 0, 256, 16), ALU.subtract)
+    both_lists(0, 0)
+
     for t in range(4):
         lower = rank < (rank ^ STEPS[t])
-        zt, zk = T["z%d" % t], ["z%d_%d" % (t, q) for q in range(4)]
-        GT, GP, Y = T["GT%d" % t], T["GP%d" % t], T["Y%d" % t]
+        zt, GT, GP, Y, JJ = "z%d" % t, "GT%d" % t, "GP%d" % t, "Y%d" % t, "JJ%d" % t
         todo = list(range(16))
 
         def max_scan(n):
             for c in todo[:n]:
-                scan(T.PM[:, 256 * c:256 * c + 256], T.mask[:], T.xg[:, 256 * c:256 * c + 256], ALU.mult, ALU.max, ["mask", "xg%d" % c], ["PM%d" % c])
+                scan(C("PM", 256 * c, 256 * c + 256), A("mk"), C("xg", 256 * c, 256 * c + 256), ALU.min, ALU.max, LOW)
             del todo[:n]
 
-        def pick_s(j):
-            c0, c1 = CH[j][0], CH[j][1] - (NV if j == JV else 0)
-            for c0, c1 in ((c0, c1),) if j < 3 else ((c0, c0 + 2), (c0 + 2, c1)):
-                act(T.xg[:, 256 * c0:256 * c1], T.X[:, 0:4096].indirect(T.hh[:, 16 * c0:16 * c1]), ACT.Copy, ["X"] + hk(j), units("xg", c0, c1))
-        for j in PARTS[0][0]:
-            pick_s(j)
-        picks(t, PARTS[1])
-        if t == 0:
-            late_constants()
-        zoff = 192.0
+        NV = PAR["NV"][t]
+        H0 = 16 * PAR["H0"]
+        cut = (0, H0, 256)
+        for c0, c1 in ((0, 4), (4, 8), (8, 12), (12, 14), (14, 16)):
+            c1 -= NV if c0 == 4 * PAR["VC"][t] else PAR["N2"][t] if c0 == 8 else 0
+            act(C("xg", 256 * c0, 256 * c1), records(c0, c1))
         for j in range(16):
             at = 64 * (j // 4) + j % 4
-            mat(T.pD[:, at:at + 61:4], IDN, zt[:, 16 * j:16 * j + 16], False, j == 15, ["IDN"] + zk, ["zP"], "D")
-        for a in range(16):
-            mat(T.pG[:, 256:272], T.WSEL[:, 15 - a:143 - a], zt[:, a:256:16], a == 0, a == 15, ["WSEL"] + zk, ["uL", "pe"], "G")
-        for tb_, b in ((T.pF, "F"), (T.pH, "H")):
-            mat(tb_[:, 0:128], T.C17[0:32, :], T.ONE[0:32, 0:128], True, False, ["C17", "ones"], ["Tp" + b], b)
+            mat(C("pA", at, at + 61, 4), IDN, C(zt, 16 * j, 16 * j + 16), True, True)
+        mat(C("pB", 0, H0), A("C17", rows=K32), C("ONE", 0, H0, rows=K32), True, False)
+        for r in range(4):
+            to, at = C("zq", r, 64, 4), C(zt, 192 + 16 * r, 208 + 16 * r)
+            op("G", lambda to=to, at=at: g.affine_select(to[0], at[0], [[0, 16]], ALU.is_ge, 0.0, 0, 0), [at], [to])
+        mat(C("pD", 0, 256 - H0), A("C17", rows=K32), C("ONE", 0, 256 - H0, rows=K32), True, False)
+
+        def u_small():
+            for a in range(16):
+                mat(C("pC", 256, 272), C("WSEL", 15 - a, 143 - a), C(zt, a, 256, 16), a == 0, a == 15)
+        if sum(PAR["G1"]):
+            u_small()
+        for hf, bank in enumerate(("pG", "pH")):
+            for k in range(16):
+                mat(C(bank, k, 512, 16), IDN, C("zq", 32 * hf, 32 * hf + 32), True, True)
 
         gpos, tpos = (0, 32) if lower else (32, 0)
-        Gs = [(T.pC, 256, 1), (T.pC, 1, 2), (T.pC, 257, 2), (T.pC, 1, 2)]
-        Go = [(T.pC, 0), (T.pC, 256), (T.pC, 0), (GT, gpos)]
-        Ts = [(T.TS, 0, 1), (T.TS, 257, 2), (T.TS, 513, 2), (T.TS, 641, 2)]
-        To = [(T.TS, 256), (T.TS, 512), (T.TS, 640), (GT, tpos)]
-        Ks = [(T.KT, 0, 1), (T.KS, 1, 2), (T.KS, 257, 2), (T.KS, 385, 2)]
-        Ko = [(T.KS, 0), (T.KS, 256), (T.KS, 384), (T.KS, 448)]
+        Gs = [("pF", 256, 1), ("pF", 1, 2), ("pF", 257, 2), ("pF", 1, 2)]
+        Go = [("pF", 0), ("pF", 256), ("pF", 0), (GT, gpos)]
+        Ts = [("TS", 0, 1), ("TS", 257, 2), ("TS", 513, 2), ("TS", 641, 2)]
+        To = [("TS", 256), ("TS", 512), ("TS", 640), (GT, tpos)]
+        Ks = [("KT", 0, 1), ("KS", 1, 2), ("KS", 257, 2), ("KS", 385, 2)]
+        Ko = [("KS", 0), ("KS", 256), ("KS", 384), ("KS", 448)]
         cpos = (0, 256, 384, 448)
 
         def prefix_t(h):
-            b = "FH"[h]
-            scan(T.TS[:, 128 * h:128 * h + 128], T.mask[:, 0:128], T["p" + b][:, 0:128], ALU.mult, ALU.add, ["mask", "Tp" + b], ["TS0_%d" % h], b)
+            n = cut[h + 1] - cut[h]
+            scan(C("TS", cut[h], cut[h + 1]), C("mask", 0, n), C("pB" if h == 0 else "pD", 0, n), ALU.mult, ALU.add)
 
         def prefix_g(h):
-            b = "EG"[h]
-            scan(T.pC[:, 256 + 128 * h:384 + 128 * h], T.mask[:, 0:128], T["p" + b][:, 0:128], ALU.mult, ALU.add,
-                 ["mask", "Gp" + b], ["C1_%d" % h], b + "C")
+            n = cut[h + 1] - cut[h]
+            scan(C("pF", 256 + cut[h], 256 + cut[h + 1]), C("mask", 0, n), C("pC" if h == 0 else "pE", 0, n), ALU.mult, ALU.add)
 
         def level(lv, h, f1, f2):
-            m, at = (128, 128 * h) if lv == 0 else (256 >> lv, 0)
+            m, at = (cut[h + 1] - cut[h], cut[h]) if lv == 0 else (256 >> lv, 0)
 
             def view(src, first, step):
                 lo = src[1] + at * src[2]
-                return src[0][:, lo + first * src[2]:lo + (m - 1) * src[2] + 1:src[2] * step]
+                return C(src[0], lo + first * src[2], lo + (m - 1) * src[2] + 1, src[2] * step)
 
             def out(dst):
-                return dst[0][:, dst[1] + at:dst[1] + at + m]
-            gk = (["C1_%d" % h], C0K, ["C1_0"], C0K)[lv]
-            gw = (C0K[2 * h:2 * h + 2], ["C1_0"], C0K, ["GTg%d" % t])[lv]
-            tk = (["TS0_%d" % h], ["TS1_0", "TS1_1"], ["TS2_0"], ["TS3_0"])[lv]
-            kk = (["KT"], ["KS1_0", "KS1_1"], ["KS2_0"], ["KS3_0"])[lv]
-            ck = "cb%d" % lv
-            c = T.cb[:, cpos[lv] + at:cpos[lv] + at + m]
-            tt(T.pA[:, 256:256 + m // 2], view(Gs[lv], 1, 2), view(Ts[lv], 0, 2), ALU.mult, gk + tk, ["p1", "zxA"], "AC")
-            tt(T.p2[:, 0:m // 2], view(Gs[lv], 0, 2), view(Ts[lv], 1, 2), ALU.mult, gk + tk, ["p2"], "C")
-            max_scan(f1)
-            tt(T.cb[:, cpos[lv] + at + 1:cpos[lv] + at + m:2], T.pA[:, 256:256 + m // 2], T.p2[:, 0:m // 2], ALU.is_gt,
-               ["p1", "p2"], [ck], "A")
-            max_scan(f2)
-            scan(out(Go[lv]), c, view(Gs[lv], 0, 1), ALU.add, ALU.min, [ck] + gk, gw, "C")
-            scan(out(To[lv]), c, view(Ts[lv], 0, 1), ALU.add, ALU.min, [ck] + tk, ["TS%d_%d" % (lv + 1, h) if lv < 3 else "GTt%d" % t])
+                return C(dst[0], dst[1] + at, dst[1] + at + m)
+            c = C("cb", cpos[lv] + at, cpos[lv] + at + m)
+            p1 = C("pA", 384, 384 + m // 2)
+            tt(p1, view(Gs[lv], 1, 2), view(Ts[lv], 0, 2), ALU.mult)
+            tt(C("p2", 0, m // 2), view(Gs[lv], 0, 2), view(Ts[lv], 1, 2), ALU.mult)
+            f1()
+            tt(C("cb", cpos[lv] + at + 1, cpos[lv] + at + m, 2), p1, C("p2", 0, m // 2), ALU.is_gt)
+            f2()
+            scan(out(Go[lv]), c, view(Gs[lv], 0, 1), ALU.add, ALU.min)
+            scan(out(To[lv]), c, view(Ts[lv], 0, 1), ALU.add, ALU.min)
             if lv == 3:
-                send(t, "G", "GT%d" % t, ["GTg%d" % t, "GTt%d" % t])
-            scan(out(Ko[lv]), c, view(Ks[lv], 0, 1), ALU.add, ALU.min, [ck] + kk, ["KS%d_%d" % (lv + 1, h)])
+                send(t, "G", GT)
+            scan(out(Ko[lv]), c, view(Ks[lv], 0, 1), ALU.add, ALU.min)
 
-        for j in PARTS[1][0]:
-            pick_s(j)
-        cp(T.z3c[:], T.pD[:, 192:256], ["zP"], ["z3c"], "D")
-        if NV:
-            c0, c1 = CH[JV][1] - NV, CH[JV][1]
-            cp(T.xg[:, 256 * c0:256 * c1], T.X[:, 0:4096].indirect(T.hh[:, 16 * c0:16 * c1]), ["X"] + hk(JV), units("xg", c0, c1))
-        for j, (c0, c1) in enumerate(CH):
-            bt, bg, at = "FH"[j // 2], "EG"[j // 2], 64 * (j % 2)
-            lo, hi = 256 * c0, 256 * c1
-            if j == 3:
-                for h, b in enumerate("AB"):
-                    xk = units("xg", c0 + 2 * h, c0 + 2 * h + 2)
-                    for a in range(8 * h, 8 * h + 8):
-                        mat(T["p" + bt][:, at:at + 64], T.SEL[:, 15 - a:143 - a], T.xg[:, lo + 64 * a:lo + 64 * a + 64], False,
-                            a == 15, ["SEL"] + xk, ["Tp" + bt], bt)
-                    tt(T.mm[:, lo + 512 * h:lo + 512 * h + 512], T.xg[:, lo + 512 * h:lo + 512 * h + 512], T["p" + b][:, 0:512], ALU.min,
-                       ["zx" + b] + xk, ["mm3_%d" % h], b)
-                    for a in range(8 * h, 8 * h + 8):
-                        mat(T["p" + bg][:, at:at + 64], T.SEL[:, 15 - a:143 - a], T.mm[:, lo + 64 * a:lo + 64 * a + 64], a == 0, a == 15,
-                            ["SEL", "mm3_%d" % h], ["Gp" + bg], bg)
-                continue
+        gaps = [lambda: cp(C("si", 0, 16), C("pC", 256, 272)),
+                lambda: ts(C("si", 16, 32), C("si", 0, 16), 15, ALU.bitwise_and),
+                lambda: tt(C("sm", 0, 16), C("si", 16, 32), i16, ALU.add),
+                lambda: cp(lsC, C("sm", 0, 16)),
+                lambda: tt(C("F0", 33, 64, 2), C("sm", 0, 16), dmp if t < 3 else dmp3x, ALU.subtract)]
+
+        def gap():
+            if todo:
+                max_scan(1)
+            elif gaps:
+                gaps.pop(0)()
+        for j in range(4):
+            c0, c1, h = 4 * j, 4 * j + 4, int(64 * j >= H0)
+            bt, bg, lo = ("pB", "pD")[h], ("pC", "pE")[h], 64 * j - cut[h]
+            x0 = 256 * c0
             for a in range(16):
-                mat(T["p" + bt][:, at:at + 64], T.SEL[:, 15 - a:143 - a], T.xg[:, lo + 64 * a:lo + 64 * a + 64], False,
-                    j % 2 == 1 and a == 15, ["SEL"] + units("xg", c0, c1), ["Tp" + bt], bt)
-            if j == 0:
-                for h, b in enumerate("AB"):
-                    for k in range(16):
-                        mat(T["p" + b][:, k:512:16], IDN, T.z3c[:, 32 * h:32 * h + 32], True, True, ["IDN", "z3c"],
-                            ["zx" + b, "U" + b, "o" + b], b)
-            for k in range(16):
-                tt(T.mm[:, lo + k:hi:16], T.xg[:, lo + k:hi:16], T.pD[:, 16 * c0:16 * c1], ALU.min,
-                   ["zP"] + units("xg", c0, c1), ["mm%d_%d" % (j, k)], "D")
-            for a in range(16):
-                mat(T["p" + bg][:, at:at + 64], T.SEL[:, 15 - a:143 - a], T.mm[:, lo + 64 * a:lo + 64 * a + 64], a == 0, a == 15,
-                    ["SEL"] + ["mm%d_%d" % (j, k) for k in range(16)], ["Gp" + bg], bg)
-            if j == 0:
-                cp(T.si[:, 0:16], T.pG[:, 256:272], ["uL"], ["si0"], "G")
-            if j == 1:
-                ts(T.si[:, 16:32], T.si[:, 0:16], 15, None, ALU.bitwise_and, None, ["si0"], ["si1"])
-                max_scan(NE)
-            if j == 2:
-                prefix_g(0)
-                prefix_t(0)
-                tt(T.sm[:, 0:16], T.si[:, 16:32], i16, ALU.add, ["si1", "i16"], ["sm0"])
-                if EARLY:
-                    level(0, 0, 1, 1)
-                cp(lsC, T.sm[:, 0:16], ["sm0"], ["lsC"])
-        if not EARLY:
-            level(0, 0, 1, 1)
-        prefix_t(1)
-        max_scan(NT)
-        act(T.XV[:, 0:256], T.X[:, 0:4096].indirect(lsC), ACT.Identity, ["X", "lsC"], ["XVo"], bias=192.0)
-        act(T.Q2[:, 0:256], zt[:], ACT.Identity, zk, ["Q2"], bias=-0.25 - zoff / 2, scale=0.5)
-        if t == 3:
-            for j, (bank, b) in enumerate(((T.pB, "B"), (T.pE, "E"), (T.pF, "F"), (T.pB, "B"))):
-                col = 512 * j
-                mat(bank[:, 0:512], IDN, T.X[:, col:col + 512], True, False, ["IDN", "X"], ["o" + b], b)
-                mat(bank[:, 0:512], SIXT, T.X[:, 2048 + col:2048 + col + 512], False, True, ["SIXT", "X"], ["o" + b], b)
-                act(T.YX[:, col:col + 512], bank[:, 0:512], ACT.Copy, ["o" + b], ["YX"], b)
-        prefix_g(1)
-        tt(T.F0[:, 65:96:2], T.sm[:, 0:16], dmp if t < 3 else dmp3x, ALU.subtract, ["sm0", "dmp", "dmp3x", "dmp3y"], ["Dl"])
-        for lv in range(4):
-            ng = NG if route(T, topo, rank, t, "Y")[0] is None else 8
-            level(lv, 1 if lv == 0 else 0, 1 if 7 - 2 * lv <= ng else 0, 1 if 8 - 2 * lv <= ng else 0)
-        Kb = T.KS[:, 449:480:2]
-        if t < 3:
-            u_start()
-        max_scan(1)
-        ts(lsY, Kb, 4096.0, None, ALU.mult, None, ["KS4_0"], ["lsY"])
-        if route(T, topo, rank, t, "Y")[0] is None:
-            rival_part(t, range(16 - LATE1, 16), ["lsY"])
-        max_scan(max(0, len(todo) - 4))
-        act(Y[:, 0:192], T.PM[:, 0:3072].indirect(T.ls[:, 0:12]), ACT.Copy, units("PM", 0, 12) + ["lsY"], ["Ya%d" % t], scale=0.5)
-        max_scan(4)
-        tt(T.sm[:, 16:32], Kb, kb0, ALU.subtract, ["KS4_0", "kb0"], ["b1"])
-        ts(Y[:, 192:256], T.PM[:, 0:4096].indirect(T.ls[:, 12:16]), 0.5, None, ALU.mult, None, units("PM", 0, 16) + ["lsY"], ["Yb%d" % t])
-        yk = ["Ya%d" % t, "Yb%d" % t]
-        send(t, "Y", "Y%d" % t, yk)
-        ts(T.F0[:, 33:64:2], T.sm[:, 16:32], 2.0 ** 19, None, ALU.mult, None, ["b1", "F0c"], ["b256"])
-        if t == 3:
-            cp(T.F1[:, 65:96:2], dmp3, ["dmp3"], ["F1x"])
-        mat(T.pG[:, 256:512], HALF, T.XV[:, 0:256], True, False, ["HALF", "XVo"], ["pe", "oG"], "G")
-        mat(T.pG[:, 256:512], IDN, Y[:], False, True, ["IDN"] + yk, ["pe"], "G")
-        mat(T.pH[:, 256:512], IDN, zt[:], True, False, ["IDN"] + zk, ["pd", "oH"], "H")
-        mat(T.pH[:, 256:512], NEG2, Y[:], False, True, ["NEG2"] + yk, ["pd"], "H")
-        act(T.XV[:, 256:512], T.pG[:, 256:512], ACT.Identity, ["pe"], ["XVn"], "G", bias=95.75)
-        if route(T, topo, rank, t, "Y")[0] is not None:
-            rival_part(t, range(16 - LATE, 16), ["XVn"])
-        act(T.ab[:], T.pH[:, 256:512], ACT.Abs, ["pd"], ["ab"], "H", bias=-zoff)
-        for b in "EF":
-            mat(T["p" + b][:, 0:128], T.C6[0:32, :], T.ONE[0:32, 0:128], True, False, ["C6", "ones"], ["pz" + b], b)
-        if t == 3:
-            ts(T.ls[:, 80:88], T.sm[:, 8:16], -2048.0, None, ALU.add, None, ["sm0"], ["lsH"])
-            tt(T.dl[:, 0:256], T.XV[:, 256:512], T.XV[:, 0:256], ALU.subtract, ["XVo", "XVn"], ["dl"])
-        ts(T.R2[:, 256:512], T.ab[:], 1.0, 192.0, ALU.max, ALU.add, ["ab"], ["zW"])
-        if t == 3:
-            tt(T.sv[:, 0:128], T.YX[:, 0:2048].indirect(T.ls[:, 16:24]), T.dl[:, 0:128], ALU.add, ["YX", "lsC", "dl"], ["sva"])
-            ts(T.dl[:, 256:384], T.dl[:, 128:256], 16.0, None, ALU.mult, None, ["dl"], ["dl16"])
-        tt(T.sm[:, 32:64], GT[:, 1:64:2], GP[:, 1:64:2], ALU.mult, ["GTg%d" % t, "GTt%d" % t, "GP%d" % t], ["pr"])
-        for j in range(3):
-            win = T.F1[:, 32 * j:32 * j + 32:2]
-            if lower:
-                tt(win, T.sm[:, 32:48], T.sm[:, 48:64], ALU.is_ge, ["pr"], ["win%d" % j])
+                mat(C(bt, lo, lo + 64), C("SEL", 15 - a, 143 - a), C("xg", x0 + 64 * a, x0 + 64 * a + 64), False, 64 * j + 64 == cut[h + 1] and a == 15)
+            if j < 3:
+                for k in range(16):
+                    tt(C("mm", x0 + k, x0 + 1024, 16), C("xg", x0 + k, x0 + 1024, 16), C("pA", 16 * c0, 16 * c1), ALU.min)
             else:
-                tt(win, T.sm[:, 48:64], T.sm[:, 32:48], ALU.is_gt, ["pr"], ["win%d" % j])
-        scan(T.F2[:], T.F0[:], T.F1[:], ALU.mult, ALU.add, ["win0", "win1", "win2", "F0c", "F1c", "F1x", "Dl", "b256"], ["F2"])
+                tt(C("mm", x0, x0 + 512), C("xg", x0, x0 + 512), A("pG"), ALU.min)
+                prefix_t(0)
+                prefix_g(0)
+                n0 = len(ops)
+                gap()
+                level(0, 0, gap, gap if PAR["LB"] > 5 else lambda: None)
+                held = ops[n0 + PAR["LB"]:]
+                del ops[n0 + PAR["LB"]:]
+                tt(C("mm", x0 + 512, x0 + 1024), C("xg", x0 + 512, x0 + 1024), A("pH"), ALU.min)
+            for a in range(16):
+                mat(C(bg, lo, lo + 64), C("SEL", 15 - a, 143 - a), C("mm", x0 + 64 * a, x0 + 64 * a + 64), a == 0, a == 15)
+            if j == PAR["J2"] and PAR["N2"][t]:
+                cp(C("xg", 256 * (12 - PAR["N2"][t]), 3072), records(12 - PAR["N2"][t], 12))
+            if j < 3:
+                for n in range(PAR["S1"][j]):
+                    max_scan(1)
+                    if n < PAR["G1"][j] and gaps:
+                        gaps.pop(0)()
+        act(A("zr"), A(zt), ACT.Relu, bias=-1.75)
+        early = len(gaps) < 2
+        if early:
+            act(C("XV", 0, 256), pick(C("X", 0, 4096), lsC), bias=192.0)
+        if not sum(PAR["G1"]):
+            u_small()
+        ops.extend(held[:-1])
+        prefix_t(1)
+        ops.extend(held[-1:])
+        max_scan(PAR["NT"])
+        prefix_g(1)
+        PZ = ((0, NA, "pG", 0), (NA, 256, "pH", 0))
+        for lo, hi, bank, at in PZ:
+            mat(C(bank, at + lo, at + hi), HALF, C("zr", lo, hi), True, False)
         if t < 3:
-            tt(T.wb[:], T.F1[:, 0:32:2], T.sm[:, 16:32], ALU.mult, ["win0", "b1"], ["wb"])
-        cp(T.ls[:, 32:80], T.F2[:, 1:96:2], ["F2"], ["lsW", "lsJ", "lsX"])
-        choose(0)
+            u_start("pB", 0, 256, True)
+            u_start("pE", NA, 256, True)
+        else:
+            for j, bank in enumerate(("pB", "pE", "pB", "pE")):
+                col, at = 512 * j, 512 * j + 128 * (j // 2)
+                mat(A(bank), IDN, C("X", col, col + 512), True, False)
+                mat(A(bank), SIXT, C("X", 2048 + col, 2560 + col), False, True)
+                act(C("YX", at, at + 512), A(bank))
+        gap()
+        for lv in range(4):
+            level(lv, 1 if lv == 0 else 0, gap, gap)
+        Kb = C("KS", 449, 480, 2)
+        gap()
+        ts(lsY, Kb, 4096.0, ALU.mult)
+        YS = PAR["YS"]
+        if split(t):
+            act(C(Y, 0, NA), pick(C("PM", 0, 16 * NA), C("ls", 0, NA // 16)), scale=0.5)
+            send(t, "Y", Y)
+            max_scan(len(todo) - (16 - YS))
+            act(C(Y, NA, 16 * YS), pick(C("PM", 0, 256 * YS), C("ls", NA // 16, YS)), scale=0.5)
+            max_scan(16)
+        else:
+            max_scan(16)
+            act(C(Y, 0, 16 * YS), pick(C("PM", 0, 256 * YS), C("ls", 0, YS)), scale=0.5)
+        tt(C("sm", 16, 32), Kb, cj, ALU.add)
+        ts(C(Y, 16 * YS, 256), pick(A("PM"), C("ls", YS, 16)), 0.5, ALU.mult)
+        send(t, "Z" if split(t) else "Y", Y)
+        rival_part(t, range(16 - late(t), 16), [A(Y)])
+
+        def splice():
+            tab = A("Tab", key="TabA")[1] + A("Tab", key="TabB")[1]
+            for h in range(2):
+                ts(C("Jw", 128 * h, 128 * h + 128), pick((T.Tab[:], tab), C("ls", 64 + 8 * h, 72 + 8 * h)), 4095 << (12 * h), ALU.bitwise_and)
+            for lo, hi, _, at in PARTS:
+                cp(C(JJ, at, at + hi - lo), C("Jw", lo, hi))
+
+        def q_win(parts):
+            for lo, hi, _, at in parts if t < 3 else ():
+                tt(C("Q2", at, at + hi - lo), C("pB", lo, hi), C("Jw", lo, hi), ALU.mult)
+
+        def first_calls():
+            ts(lsJ, C("sm", 16, 32), 2.0 ** 19, ALU.mult)
+            tt(A("b1"), Kb, kb0, ALU.subtract)
+            if JW == 0:
+                splice()
+
+        def rest_gaps():
+            while gaps:
+                gaps.pop(0)()
+        JW, QW = PAR["JW"][t], PAR["QW"][t]
+        mat(C("pD", 256, 512), IDN, A(zt), True, False)
+        mat(C("pD", 256, 512), NEG2, A(Y), False, True)
+        act(A("ab"), C("pD", 256, 512), ACT.Abs)
+        n0 = len(ops)
+        weave(rest_gaps, first_calls)
+        behind = ops[n0 + PAR["ZW"]:]
+        del ops[n0 + PAR["ZW"]:]
+        for lo, hi, _, at in PARTS:
+            ts(C("Z2", at, at + hi - lo), C("ab", lo, hi), 1.0, ALU.max, 192.0, ALU.add)
+        ops.extend(behind)
+        if not early:
+            act(C("XV", 0, 256), pick(C("X", 0, 4096), lsC), bias=192.0)
         if t < 3:
-            splice(t, 0)
-            tt(T.X[:, 0:4352].indirect(T.ls[:, 64:64 + CUT]), T.XV[:, 256:256 + 16 * CUT], T.m192[:, 0:16 * CUT], ALU.add,
-               ["XVn", "m192", "lsX"], ["X"])
-            mat(T.pG[:, 0:16], T.BIG[:], T.wb[:], True, True, ["BIG", "wb"], ["pa"], "G")
-            act(T.junk[:], T.pG[:, 0:16], ACT.Copy, ["pa"], ["junk", "A32"], "G", accum_out=T.A32[:, 0:1])
-        choose(1)
+            u_start("pD", 0, NA, True)
+            for lo, hi, _, at in PARTS:
+                mat(C("pF", lo, hi), W2, C("Z2", at, at + hi - lo), True, True)
+            for lo, hi, _, at in PARTS:
+                u_sum("pB", lo, hi, "Z2", at)
+            u_cast("pF", 0, 256, "tw", True)
+        mat(C("pC", 256, 512), HALF, C("XV", 0, 256), True, False)
+        mat(C("pC", 256, 512), IDN, A(Y), False, True)
+        act(C("XV", 256, 512), C("pC", 256, 512), bias=95.75)
         if t < 3:
-            demand(t, 0)
-            tt(T.X[:, 0:4352].indirect(T.ls[:, 64 + CUT:80]), T.XV[:, 256 + 16 * CUT:512], T.m192[:, 16 * CUT:256], ALU.add,
-               ["XVn", "m192", "lsX"], ["X"])
-            picks(t + 1, PARTS[0])
-            demand(t, 1)
-            splice(t, 1)
-            names_out(t + 1)
-    cp(T.YX[:, 0:2304].indirect(T.ls[:, 64:72]), T.sv[:, 0:128], ["sva", "lsX"], ["YX"])
-    tt(T.sv[:, 128:256], T.YX[:, 0:2048].indirect(T.ls[:, 80:88]), T.dl[:, 256:384], ALU.add, ["YX", "lsH", "dl16"], ["svb"])
-    cp(T.YX[:, 0:2304].indirect(T.ls[:, 72:80]), T.sv[:, 128:256], ["svb", "lsX"], ["YX"])
-    dma("Y", T.yx[:], T.YX[:, 0:2048], "out2", ["YX"], ())
-    splice(3, 0)
-    demand(3, 0)
-    demand(3, 1)
-    splice(3, 1)
-    act(T.tb[:], T.z4[:], ACT.Identity, ["z4_%d" % q for q in range(4)], ["tb%d" % q for q in range(4)], bias=-192.0)
-    dma("S", T.yz[:], T.tb[:], "out4", ["tb0"], ())
-    cp(T.KS[:, 0:128], T.J4[:, 0:128], ["J4A"], ["KS1_0"])
-    ts(T.KS[:, 128:256], T.J4[:, 128:256], 2.0 ** -12, None, ALU.mult, None, ["J4B"], ["KS1_1"])
-    dma("Y", T.yj[:], T.KS[:, 0:256], "out1", ["KS1_0", "KS1_1"], ())
+            u_rest("pB", 0, 256, "tw")
+        else:
+            cp(C("F1", 33, 64, 2), dmp3)
+            tt(C("sm", 64, 80), C("F0", 33, 64, 2), dmp3, ALU.add)
+            tt(C("dl", 0, 256), C("XV", 256, 512), C("XV", 0, 256), ALU.subtract)
+            cp(C("ls", 80, 96), C("sm", 64, 80))
+            ts(C("dl", 256, 384), C("dl", 128, 256), 16.0, ALU.mult)
+            for h in range(2):
+                tt(C("sv", 64 * h, 64 * h + 64), pick(yx(h), C("ls", 80 + 4 * h, 84 + 4 * h)), C("dl", 64 * h, 64 * h + 64), ALU.add)
+        if JW == 1:
+            splice()
+        if QW == 0:
+            q_win(PARTS)
+        tt(C("sm", 32, 64), C(GT, 1, 64, 2), C(GP, 1, 64, 2), ALU.mult)
+        for j in range(2):
+            win = C("F1", 32 * j, 32 * j + 32, 2)
+            if lower:
+                tt(win, C("sm", 32, 48), C("sm", 48, 64), ALU.is_ge)
+            else:
+                tt(win, C("sm", 48, 64), C("sm", 32, 48), ALU.is_gt)
+        if t < 3:
+            tt(A("wb"), C("F1", 0, 32, 2), A("b1"), ALU.mult)
+        scan(A("F2"), A("F0"), A("F1"), ALU.mult, ALU.add)
+        if QW == 1:
+            q_win(PARTS[:1])
+        cp(C("ls", 32, 64), C("F2", 1, 64, 2))
+        if QW == 1:
+            q_win(PARTS[1:])
+        if t == 3:
+            def low(h):
+                cp(pick(yx(h, 128), C("ls", 48 + 4 * h, 52 + 4 * h)), C("sv", 64 * h, 64 * h + 64))
+
+            def high(h):
+                tt(C("sv", 128 + 64 * h, 192 + 64 * h), pick(yx(h), C("ls", 88 + 4 * h, 92 + 4 * h)), C("dl", 256 + 64 * h, 320 + 64 * h), ALU.add)
+                cp(pick(yx(h, 128), C("ls", 56 + 4 * h, 60 + 4 * h)), C("sv", 128 + 64 * h, 192 + 64 * h))
+                dma("Y", C("yx", 1024 * h, 1024 * h + 1024), C("YX", 1152 * h, 1152 * h + 1024), "out%d" % (2 + h))
+            low(0)
+            low(1)
+            high(0)
+            high(1)
+            if JW == 2:
+                splice()
+
+        def names(parts):
+            for lo, hi, at, _ in parts:
+                act(C("JJ%d" % (t + 1), at, at + hi - lo), pick(A(JJ), C("ls", 32 + lo // 16, 32 + hi // 16)))
+        if t < 3:
+            mat(C("pA", 256, 272), A("BIG"), A("wb"), True, True)
+            act(A("junk"), C("pA", 256, 272), acc=A32)
+            JE = PAR["JE"][t]
+            names(PARTS[:JE])
+
+        def names_store():
+            act(C("Jo", 0, 128), pick(A(JJ), C("ls", 32, 40)))
+            act(C("Jo", 128, 256), pick(A(JJ), C("ls", 40, 48)), scale=2.0 ** -12)
+            dma("S", A("yj"), A("Jo"), "out1")
+        if t == 3 and JW < 2:
+            names_store()
+
+        def z_lose(part):
+            (lo, hi, bank, at), to = PZ[part], PARTS[part][2]
+            mat(C(bank, at + lo, at + hi), IDN, C("YP%d" % t, lo, hi), False, True)
+            act(C("Z2", to, to + hi - lo), C(bank, at + lo, at + hi), bias=192.4375)
+        z_lose(0)
+        z_lose(1)
+        if t < 3:
+            if PAR["JM"][t]:
+                factors("Z2", (0, 2 * NA), (0,))
+                names(PARTS[JE:])
+                factors("Z2", (0, 2 * NA), (1,))
+            else:
+                factors("Z2", (0, 2 * NA), (0, 1))
+                names(PARTS[JE:])
+        act(A("z%d" % (t + 1)), pick(A("Z2"), lsW), bias=-192.0)
+        if t < 3:
+            tt(pick(A("X"), lsX), C("XV", 256, 512), A("m192"), ALU.add)
+            if QW == 2:
+                q_win(PARTS)
+            both_lists(t + 1, t)
+    dma("S", A("yz"), A("z4"), "out4")
+    if JW == 2:
+        names_store()
     emit(g, T, ops, left[0])
 
 

import numpy as np
from concourse.mybir import AluOpType as ALU, ActivationFunctionType as ACT

STEPS = (4, 1, 6, 3)
PAR = {
    "NV": (3, 2, 2, 2),
    "S1": (2, 1, 0),
    "G1": (0, 0, 0),
    "H0": 8,
    "JE": (2, 2, 2),
    "JM": (0, 0, 0),
    "PK": (0, 0, 0),
    "LB": 5,
    "ZW": 7,
    "CA": 0,
    "ORD": ((0, 0), (0, 1), (0, 2), (1, 0), (0, 3), (1, 1), (1, 2), (1, 3)),
    "VC": (0, 1, 1, 1),
    "N2": (0, 0, 0, 0),
    "J2": 1,
    "NT": 0,
    "NG": 8,
    "YS": 12,
    "CUT": 16,
    "YSPLIT": (0, 0, 0, 0),
    "DB": (0, 15),
    "JW": (0, 0, 0, 0),
    "QW": (1, 1, 1, 0),
    "GN": 16,
    "LATE": (0, 0),
}
CH = ((0, 4), (4, 8), (8, 14), (14, 16))
NA = 64
C0 = 327680.0
LOW = 0.375

SCRATCH = {
    "X": ("sbuf", [128, 4352], "bfloat16"),
    "xg": ("sbuf", [128, 4096], "bfloat16"),
    "mm": ("sbuf", [128, 4096], "bfloat16"),
    "zq": ("sbuf", [128, 64], "bfloat16"),
    "PM": ("sbuf", [128, 4096], "bfloat16"),
    "Tab": ("sbuf", [128, 2048], "int32"),
    "D": ("dram", [8, 4096], "int32"),
    "Ji": ("sbuf", [128, 256], "int32"),
    "wc": ("sbuf", [128, 1], "float32"),
    "BD": ("sbuf", [128, 128], "bfloat16"),
    "BD1": ("sbuf", [128, 128], "bfloat16"),
    "W2": ("sbuf", [128, 256], "bfloat16"),
    "SEL": ("sbuf", [128, 144], "bfloat16"),
    "WSEL": ("sbuf", [128, 144], "bfloat16"),
    "ID": ("sbuf", [128, 768], "bfloat16"),
    "CL": ("sbuf", [128, 128], "bfloat16"),
    "C17": ("sbuf", [128, 128], "bfloat16"),
    "BIG": ("sbuf", [128, 128], "bfloat16"),
    "ip": ("sbuf", [128, 2], "int32"),
    "acol": ("sbuf", [128, 2], "float32"),
    "KT": ("sbuf", [128, 256], "float32"),
    "iL": ("sbuf", [128, 128], "float32"),
    "mask": ("sbuf", [128, 192], "bfloat16"),
    "mk": ("sbuf", [128, 256], "bfloat16"),
    "cb": ("sbuf", [128, 480], "bfloat16"),
    "Z2": ("sbuf", [128, 512], "bfloat16"),
    "Q2": ("sbuf", [128, 512], "float32"),
    "XV": ("sbuf", [128, 512], "bfloat16"),
    "sv": ("sbuf", [128, 256], "bfloat16"),
    "dl": ("sbuf", [128, 384], "bfloat16"),
    "ab": ("sbuf", [128, 256], "bfloat16"),
    "zr": ("sbuf", [128, 256], "bfloat16"),
    "m192": ("sbuf", [128, 256], "bfloat16"),
    "m192h": ("sbuf", [128, 256], "bfloat16"),
    "tb": ("sbuf", [128, 256], "bfloat16"),
    "tw": ("sbuf", [128, 256], "bfloat16"),
    "qi": ("sbuf", [128, 256], "int32"),
    "qj": ("sbuf", [128, 4, 64], "int32"),
    "Jw": ("sbuf", [128, 256], "int32"),
    "Jo": ("sbuf", [128, 256], "float32"),
    "ONE": ("sbuf", [128, 192], "bfloat16"),
    "ONEh": ("sbuf", [128, 256], "bfloat16"),
    "hh": ("sbuf", [128, 256], "uint16"),
    "TS": ("sbuf", [128, 704], "float32"),
    "KS": ("sbuf", [128, 480], "float32"),
    "p2": ("sbuf", [128, 128], "float32"),
    "sm": ("sbuf", [128, 96], "float32"),
    "b1": ("sbuf", [128, 16], "float32"),
    "F0": ("sbuf", [128, 64], "float32"),
    "F1": ("sbuf", [128, 64], "float32"),
    "F2": ("sbuf", [128, 64], "float32"),
    "si": ("sbuf", [128, 32], "int32"),
    "wb": ("sbuf", [128, 16], "bfloat16"),
    "ls": ("sbuf", [128, 96], "uint16"),
    "A32": ("sbuf", [128, 1], "float32"),
    "ub": ("sbuf", [128, 1], "float32"),
    "junk": ("sbuf", [128, 16], "float32"),
    "YX": ("sbuf", [128, 2304], "bfloat16"),
}
for _t in range(5):
    SCRATCH["z%d" % _t] = ("sbuf", [128, 256], "bfloat16")
for _t in range(4):
    SCRATCH["JJ%d" % _t] = ("sbuf", [128, 512], "float32")
    SCRATCH["JP%d" % _t] = ("sbuf", [128, 128], "int32")
    SCRATCH["PK%d" % _t] = ("sbuf", [128, 128], "int32")
    SCRATCH["GT%d" % _t] = ("sbuf", [128, 64], "float32")
    SCRATCH["GP%d" % _t] = ("sbuf", [128, 64], "float32")
    SCRATCH["Y%d" % _t] = ("sbuf", [128, 256], "bfloat16")
    SCRATCH["YP%d" % _t] = ("sbuf", [128, 256], "bfloat16")
for _b in "ABCDEFGH":
    SCRATCH["p" + _b] = ("psum", [128, 512], "float32")

SEMAPHORES = ["cV", "cS", "cP", "cG", "left", "ldj", "ldz", "ldw", "ldx", "out1", "out2", "out3", "out4"]
for _t in range(4):
    SEMAPHORES += ["aJ%d" % _t, "aG%d" % _t, "aY%d" % _t, "aZ%d" % _t, "dA%d" % _t, "dB%d" % _t, "tA%d" % _t, "tB%d" % _t]


def helper(T, topo, rank):
    me = T.cores[rank]
    able = [c for c in topo.cores_of(me) if T.rank_of(c) is None and all(topo.may_write(c, T.cores[rank ^ s]) for s in STEPS)]
    able.sort(key=lambda c: (topo.die(c) != topo.die(me), c))
    return able[0]


def route(T, topo, rank, t):
    me, to = T.cores[rank], T.cores[rank ^ STEPS[t]]
    if topo.may_write(me, to):
        return None, to, topo.mask(me, to), topo.mask(me, to)
    via = helper(T, topo, rank)
    return via, to, topo.mask(me, via), topo.mask(via, to)


def bits(m):
    return bin(m).count("1")


def split(t):
    return PAR["YSPLIT"][t]


def letters(t):
    ys = [("Y", "Y", 0, NA), ("Z", "Y", NA, 256)] if split(t) else [("Y", "Y", 0, 256)]
    return [("J", "J", 0, 128), ("G", "G", 0, 64)] + ys


def relay_program(g, core, T, topo):
    left = 0
    for rank in range(len(T.cores)):
        for t in range(len(STEPS)):
            via, to, m0, m = route(T, topo, rank, t)
            if via != core:
                continue
            rid, pid = topo.addr(to, core)
            for kind, name, lo, hi in letters(t):
                buf, sem = T["%sP%d" % (name, t)][:, lo:hi], T.sem["a%s%d" % (kind, t)]
                g.wait_ge(sem, bits(m0))
                g.remote_dma(buf, buf, sem, T.sem.left, pid, rid, m)
                left += bits(m)
    if left:
        g.wait_ge(T.sem.left, left)


def emit(g, T, ops, left):
    queue = {"V": g.vector, "S": g.scalar, "P": g.tensor, "G": g, "Y": g.sync}
    own = {"V": "cV", "S": "cS", "P": "cP", "G": "cG"}
    last_w, last_r, bank = {}, {}, {}
    known = {q: {} for q in queue}
    total = {}
    for o in ops:
        if o["sem"] is not None and o["q"] is not None:
            total[o["sem"]] = total.get(o["sem"], 0) + 16
    used = set()
    for n, o in enumerate(ops):
        q = o["q"]
        for name, size, at in o["r"] + o["w"]:
            if name not in last_w:
                last_w[name], last_r[name] = np.full(size, -1), {}
        banks = {name for name, size, at in o["r"] + o["w"] if name in SCRATCH and SCRATCH[name][0] == "psum"}
        if q is None:
            o["tok"], o["snap"] = (o["sem"], o["val"]), {}
        else:
            deps = set()
            for name, size, at in o["r"] + o["w"]:
                deps.update(np.unique(last_w[name][at]).tolist())
            for name, size, at in o["w"]:
                for seen in last_r[name].values():
                    deps.add(int(seen[at].max()))
            for b in banks:
                deps.update(v for qq, v in bank.get(b, {}).items() if qq != q)
            deps.discard(-1)
            need = {}
            for d in deps:
                p = ops[d]
                if p["remote"] or (q == "P" and p["q"] == "P"):
                    continue
                if o["sem"] is not None and p["sem"] == o["sem"]:
                    continue
                s, v = p["tok"]
                if s not in need or need[s][0] < v:
                    need[s] = (v, d)
            o["waits"] = []
            for s, (v, d) in sorted(need.items(), key=lambda e: -e[1][1]):
                if known[q].get(s, -1) >= v:
                    continue
                o["waits"].append(d)
                used.add(d)
                known[q][s] = v
                for s2, v2 in ops[d]["snap"].items():
                    if known[q].get(s2, -1) < v2:
                        known[q][s2] = v2
            o["snap"] = dict(known[q])
            o["tok"] = (o["sem"], total[o["sem"]]) if o["sem"] is not None else (own.get(q), n)
        for name, size, at in o["r"]:
            last_r[name].setdefault(o["sem"] or q, np.full(size, -1))[at] = n
        for name, size, at in o["w"]:
            last_w[name][at] = n
        for b in banks:
            bank.setdefault(b, {})[q] = n
    count = {s: 0 for s in own.values()}
    for n, o in enumerate(ops):
        if o["q"] is None:
            total[o["sem"]] = o["val"]
            continue
        e = queue[o["q"]]
        for d in o["waits"]:
            e.wait_ge(T.sem[ops[d]["tok"][0]], ops[d]["tok"][1])
        ins = o["f"]()
        if o["sem"] is not None:
            ins.then_inc(T.sem[o["sem"]], 16)
        elif n in used:
            s = own[o["q"]]
            count[s] += 1
            o["tok"] = (s, count[s])
            ins.then_inc(T.sem[s], 1)
    total.update(count)
    total["left"] = left
    for s, v in total.items():
        if v:
            g.wait_ge(T.sem[s], v)


def build_rank(g, core, T, topo, rank):
    ops = []
    left = [0]
    V, S, P = g.vector, g.scalar, g.tensor
    grid = {}

    def A(name, *idx, rows=slice(None), key=None):
        ap = T[name][(rows,) + idx] if idx else T[name][rows]
        if key:
            return ap, [(key, 1, np.zeros(1, int))]
        if name not in grid:
            shape = list(T[name].shape)[1:]
            grid[name] = np.arange(int(np.prod(shape))).reshape(shape)
        return ap, [(name, grid[name].size, grid[name][idx].reshape(-1))]

    def C(name, lo, hi, step=1, rows=slice(None)):
        return A(name, slice(lo, hi, step) if step > 1 else slice(lo, hi), rows=rows)

    def pick(win, off, more=()):
        return win[0].indirect(off[0]), win[1] + off[1] + list(more), off[1]

    def op(q, f, r=(), w=(), sem=None, remote=False, val=None):
        rd = [e for a in r if isinstance(a, tuple) for e in a[1]] + [e for a in w if len(a) == 3 for e in a[2]]
        wr = [e for a in w for e in (a[1] if len(a) == 2 else a[1][:1])]
        ops.append({"q": q, "f": f, "r": rd, "w": wr, "sem": sem, "remote": remote, "val": val})

    def num(x):
        return x[0] if isinstance(x, tuple) else x

    def tt(out, a, b, alu):
        op("V", lambda: V.tensor_tensor(out[0], a[0], b[0], alu), [a, b], [out])

    def ts(out, a, s1, o0, s2=None, o1=None):
        if o1 is None:
            op("V", lambda: V.tensor_scalar(out[0], a[0], num(s1), None, o0), [a, s1], [out])
        else:
            op("V", lambda: V.tensor_scalar(out[0], a[0], num(s1), num(s2), o0, o1), [a, s1, s2], [out])

    def cp(out, a):
        op("V", lambda: V.tensor_copy(out[0], a[0]), [a], [out])

    def scan(out, d0, d1, o0, o1, first=0.0):
        op("V", lambda: V.tensor_tensor_scan(out[0], d0[0], d1[0], first, o0, o1), [d0, d1], [out])

    def fill(out, v):
        op("V", lambda: V.memset(out[0], v), (), [out])

    def act(out, a, fn=ACT.Identity, bias=None, scale=None, acc=None):
        kw = {}
        if bias is not None:
            kw["bias"] = num(bias)
        if scale is not None:
            kw["scale"] = scale
        if acc is not None:
            kw["accum_out"] = acc[0]
        op("S", lambda: S.activation(out[0], a[0], fn if bias is not None or fn != ACT.Identity else ACT.Copy, **kw), [a, bias], [out] + ([acc] if acc else []))

    def mat(out, lhsT, rhs, start, stop):
        op("P", lambda: P.matmul(out[0], lhsT[0], rhs[0], start, stop), [lhsT, rhs], [out])

    def dma(q, out, a, sem, after=()):
        e = g.sync if q == "Y" else S
        op(q, lambda: e.dma_start(out[0], a[0]), [a] + list(after), [out], sem=sem)

    def send(t, kind, src):
        via, to, m, _ = route(T, topo, rank, t)
        rid, pid = topo.addr(to if via is None else via, core)
        name, lo, hi = [e[1:] for e in letters(t) if e[0] == kind][0]
        dst, sem = "%sP%d" % (name, t), "a%s%d" % (kind, t)
        left[0] += bits(m)
        op("G", lambda: g.remote_dma(T[dst][:, lo:hi], T[src][:, lo:hi], T.sem[sem], T.sem.left, pid, rid, m), [C(src, lo, hi)], (), remote=True)
        op(None, None, (), [C(dst, lo, hi)], sem=sem, val=bits(route(T, topo, rank ^ STEPS[t], t)[3]))

    def weave(*chains):
        got = []
        for fn in chains:
            n = len(ops)
            fn()
            got.append(ops[n:])
            del ops[n:]
        for k in range(max(len(c) for c in got)):
            ops.extend(c[k] for c in got if k < len(c))

    IDN, HALF, NEG2, SIXT, NEG, NEGH = (C("ID", 128 * j, 128 * j + 128) for j in range(6))
    W2, W2H = C("W2", 0, 128), C("W2", 128, 256)
    lsY, lsC, lsW, lsX, lsJ = (C("ls", 16 * j, 16 * j + 16) for j in range(5))
    lane, kb0, cj, i16, dmp, dmp3, dmp3x = (C("iL", 16 * j, 16 * j + 16) for j in range(1, 8))
    a0 = C("acol", 0, 1)
    A32 = A("A32")
    K32, K64 = slice(0, 32), slice(0, 64)
    PARTS = ((0, NA, 0, NA), (NA, 256, 2 * NA, 256 + NA))

    dma("Y", A("z0"), A("zd"), "ldz")
    dma("S", A("wc"), A("wt"), "ldw")
    dma("Y", A("Ji"), A("jn"), "ldj")
    dma("Y", C("X", 0, 4096), A("xt"), "ldx")
    fill(A("ONE"), 1.0)
    op("G", lambda: g.affine_select(T.BD1[:], T.ONE[:, 0:128], [[-16, 8], [0, 16]], ALU.is_ge, 0.0, 0, 1), [A("ONE")], [A("BD1")])
    op("G", lambda: g.affine_select(T.BD[:], T.BD1[:], [[16, 8], [0, 16]], ALU.is_ge, 0.0, 15, -1), [A("BD1")], [A("BD")])
    op("G", lambda: g.affine_select(IDN[0], T.ONE[:, 0:128], [[-1, 128]], ALU.is_equal, 0.0, 0, 1), [A("ONE")], [IDN])
    op("G", lambda: g.iota(T.ip[:, 0:1], [[0, 1]], 0, 1), (), [C("ip", 0, 1)])
    op("G", lambda: g.iota(T.iL[:, 0:16], [[16, 16]], 0, 0, allow_small_or_imprecise_dtypes=True), (), [C("iL", 0, 16)])
    op("G", lambda: g.iota(T.KT[:], [[1024, 4], [16, 4], [1, 16]], 0, 0, allow_small_or_imprecise_dtypes=True), (), [A("KT")])
    fill(A("CL", rows=K32, key="CL0"), C0 / 32)
    fill(A("CL", rows=slice(32, 64), key="CL1"), 33.0 / 32)
    CL = (T.CL[0:64, :], A("CL", key="CL0")[1] + A("CL", key="CL1")[1])
    fill(C("ONEh", 0, 128), 1.0)
    fill(C("ONEh", 128, 256), 2.0 ** -12)
    fill(A("SEL"), 0.0)
    fill(A("WSEL"), 0.0)
    fill(A("C17", rows=K32), 2.0 ** -17)
    fill(A("mask"), 1.0)
    fill(A("mk"), 99.0)
    fill(A("cb"), 1.0)
    fill(A("BIG"), 2.0 ** 17)
    fill(A("m192"), -192.0)
    fill(C("m192h", 0, 128), -192.0)
    fill(C("m192h", 128, 256), -192.0 * 2.0 ** -12)
    fill(A("F0"), 0.0)
    fill(C("mask", 0, 192, 16), 0.0)
    fill(C("mk", 0, 256, 16), LOW)
    fill(C("F0", 1, NA // 8, 2), float(NA))
    fill(C("F0", NA // 8 + 1, 32, 2), 256.0 - NA)
    ts(W2, A("BD"), A("wc"), ALU.mult, 2.0, ALU.mult)
    ts(W2H, A("BD"), A("wc"), ALU.mult, 2.0 ** -11, ALU.mult)
    ts(NEG, IDN, -1.0, ALU.mult)
    ts(NEGH, IDN, -2.0 ** -12, ALU.mult)

    def u_start(bank, lo, hi, shifted):
        mat(C(bank, lo, hi), CL, C("ONEh", lo, hi, rows=K64), True, False)
        if shifted:
            mat(C(bank, lo, hi), W2, C("m192h", lo, hi), False, False)

    def halves(lo, hi):
        return [(a, b) for a, b in ((lo, min(hi, 128)), (max(lo, 128), hi)) if a < b]

    def u_sum(bank, lo, hi, z, at):
        for a, b in halves(lo, hi):
            mat(C(bank, a, b), W2 if a < 128 else W2H, C(z, at + a - lo, at + b - lo), False, False)

    def u_cast(bank, lo, hi, tb, shifted):
        act(C(tb, lo, hi), C(bank, lo, hi), bias=A("ub") if shifted else C0 + 33 - 1056)

    def u_rest(bank, lo, hi, tb):
        for a, b in halves(lo, hi):
            mat(C(bank, a, b), NEG if a < 128 else NEGH, C(tb, a, b), False, b == hi)

    def names_pack(t):
        J = "JJ%d" % t
        for lo, at in ((0, 0), (NA, 2 * NA)):
            n = NA if lo == 0 else 128 - NA
            tt(C("PK%d" % t, lo, lo + n), C(J, at, at + n), C(J, 128 + NA + lo, 128 + NA + lo + n), ALU.add)

    def names_out(t):
        send(t, "J", "PK%d" % t)
        dma("Y", C("D", 0, 2048), A("PK%d" % t), "dA%d" % t)
        for k in range(16):
            if k == (PAR["DB"][far(t)]):
                dma("Y", C("D", 2048, 4096), A("JP%d" % t), "dB%d" % t)
            if k < 15:
                dma("Y", A("Tab", slice(0, (15 - k) * 128), rows=slice(k, 128, 16), key="TabA"), C("D", (k + 1) * 128, 2048), "tA%d" % t)
        rival_part(t, range(16 - late(t)), [])

    def far(t):
        return int(route(T, topo, rank, t)[0] is not None)

    def late(t):
        return PAR["LATE"][far(t)]

    def rival_part(t, ks, after):
        for k in ks:
            dma("Y", A("Tab", slice((15 - k) * 128, 2048), rows=slice(k, 128, 16), key="TabB"), C("D", 2048, 2048 + (k + 1) * 128), "tB%d" % t, after)

    def both_lists(t, old):
        got = []
        for part in range(2):
            n = len(ops)
            lists(t, part, old)
            got.append(ops[n:])
            del ops[n:]
        for n, (part, k) in enumerate(PAR["ORD"]):
            if t and n == PAR["PK"][old]:
                names_pack(t)
                names_out(t)
            ops.extend(got[part][k:k + 1] if k < 3 else got[part][3:])
        c1 = 4 * PAR["VC"][t] + 4
        c0 = c1 - PAR["NV"][t]
        if c0 < c1:
            cp(C("xg", 256 * c0, 256 * c1), records(c0, c1))

    def records(c0, c1):
        return pick(C("X", 0, 4096), C("hh", 16 * c0, 16 * c1))

    def lists(t, part, old):
        lo, hi, at, _ = PARTS[part]
        tt(C("Q2", at, at + hi - lo), C("pD" if part == 0 else "pE", lo, hi), C("JJ%d" % old, at, at + hi - lo), ALU.mult)
        if t == 0:
            cp(C("qi", lo, hi), C("Q2", at, at + hi - lo))
        else:
            ts(C("qi", lo, hi), pick(C("Q2", 0, 2 * hi), C("ls", 32 + lo // 16, 32 + hi // 16)), A32, ALU.add)
        js = slice(lo // 64, hi // 64)
        ts(A("qj", js), C("qi", lo, hi), 5, ALU.arith_shift_right, 4095, ALU.bitwise_and)
        for r in range(4):
            cp(C("hh", lo + r, hi, 4), A("qj", js, slice(16 * r, 16 * r + 16)))

    def factors(z, ats, parts):
        for part in parts:
            (lo, hi, _, _), at, side = PARTS[part], ats[part], ("pF", "pA")[part]
            mat(C(side, lo, hi), W2, C(z, at, at + hi - lo), True, True)
            u_sum(("pD", "pE")[part], lo, hi, z, at)
            u_cast(side, lo, hi, "tb", z == "Z2")
            if PAR["CA"]:
                u_rest(("pD", "pE")[part], PARTS[part][0], PARTS[part][1], "tb")
        for part in parts if not PAR["CA"] else ():
            u_rest(("pD", "pE")[part], PARTS[part][0], PARTS[part][1], "tb")

    def yx(h, spare=0):
        return C("YX", 1152 * h, 1152 * h + 1024 + spare)

    u_start("pD", 0, NA, False)
    u_start("pE", NA, 256, False)
    factors("z0", (0, NA), (0, 1))
    mat(C("pC", 0, 1), CL, C("ONEh", 0, 1, rows=K64), True, False)
    mat(C("pC", 0, 1), W2, C("m192h", 0, 1), False, True)
    act(A("ub"), C("pC", 0, 1), bias=-1056.0)
    ts(C("SEL", 15, 143, 16), C("BD", 0, 128, 16), 2.0 ** -12, ALU.mult)
    ts(C("WSEL", 15, 143, 16), C("BD", 0, 128, 16), A("wc"), ALU.mult)
    ts(C("ip", 1, 2), C("ip", 0, 1), 15, ALU.bitwise_and)
    ts(HALF, IDN, 0.5, ALU.mult)
    cp(a0, C("ip", 1, 2))
    ts(C("acol", 1, 2), C("ip", 1, 2), 64.0, ALU.mult)
    ts(NEG2, IDN, -2.0, ALU.mult)
    ts(lane, C("iL", 0, 16), a0, ALU.add)
    ts(A("KT"), A("KT"), C("acol", 1, 2), ALU.add, 2.0 ** -12, ALU.mult)
    ts(SIXT, IDN, 16.0, ALU.mult)
    cp(C("JJ0", 0, NA), C("Ji", 0, NA))
    cp(C("JJ0", 2 * NA, 128 + NA), C("Ji", NA, 128))
    ts(C("JJ0", 128 + NA, 256 + NA), C("Ji", 128, 256), 4096.0, ALU.mult)
    ts(i16, lane, 16.0, ALU.mult)
    names_pack(0)
    names_out(0)
    ts(C("F1", 1, NA // 8, 2), C("iL", 16, 16 + NA // 16), 0.0, ALU.add)
    ts(C("F1", NA // 8 + 1, 32, 2), C("iL", 16 + NA // 16, 32), float(NA), ALU.add)
    ts(C("F1", 33, 64, 2), lane, 4096.0, ALU.add)
    ts(dmp, lane, 4096.0, ALU.add)
    for j in range(4):
        ts(C("iL", 96 + 4 * j, 100 + 4 * j), C("iL", 16, 20), 1024.0, ALU.add)
        ts(C("iL", 112 + 4 * j, 116 + 4 * j), C("iL", 16, 20), 1024.0 * (j + 1), ALU.add)
    ts(kb0, C("KT", 0, 256, 16), -2.0 ** -12, ALU.add)
    ts(C("sm", 0, 8), C("iL", 16, 24), 2.0 ** -19, ALU.mult)
    ts(C("sm", 8, 16), C("iL", 24, 32), 2.0 ** -19, ALU.mult, -2.0 ** -12, ALU.add)
    tt(cj, C("sm", 0, 16), C("KT", 0, 256, 16), ALU.subtract)
    both_lists(0, 0)

    for t in range(4):
        lower = rank < (rank ^ STEPS[t])
        zt, GT, GP, Y, JJ = "z%d" % t, "GT%d" % t, "GP%d" % t, "Y%d" % t, "JJ%d" % t
        todo = list(range(16))

        def max_scan(n):
            for c in todo[:n]:
                scan(C("PM", 256 * c, 256 * c + 256), A("mk"), C("xg", 256 * c, 256 * c + 256), ALU.min, ALU.max, LOW)
            del todo[:n]

        NV = PAR["NV"][t]
        H0 = 16 * PAR["H0"]
        cut = (0, H0, 256)
        for c0, c1 in ((0, 4), (4, 8), (8, 12), (12, 14), (14, 16)):
            c1 -= NV if c0 == 4 * PAR["VC"][t] else PAR["N2"][t] if c0 == 8 else 0
            act(C("xg", 256 * c0, 256 * c1), records(c0, c1))
        for j in range(16):
            at = 64 * (j // 4) + j % 4
            mat(C("pA", at, at + 61, 4), IDN, C(zt, 16 * j, 16 * j + 16), True, True)
        mat(C("pB", 0, H0), A("C17", rows=K32), C("ONE", 0, H0, rows=K32), True, False)
        for r in range(4):
            to, at = C("zq", r, 64, 4), C(zt, 192 + 16 * r, 208 + 16 * r)
            op("G", lambda to=to, at=at: g.affine_select(to[0], at[0], [[0, 16]], ALU.is_ge, 0.0, 0, 0), [at], [to])
        mat(C("pD", 0, 256 - H0), A("C17", rows=K32), C("ONE", 0, 256 - H0, rows=K32), True, False)

        def u_small():
            for a in range(16):
                mat(C("pC", 256, 272), C("WSEL", 15 - a, 143 - a), C(zt, a, 256, 16), a == 0, a == 15)
        if sum(PAR["G1"]):
            u_small()
        for hf, bank in enumerate(("pG", "pH")):
            for k in range(16):
                mat(C(bank, k, 512, 16), IDN, C("zq", 32 * hf, 32 * hf + 32), True, True)

        gpos, tpos = (0, 32) if lower else (32, 0)
        Gs = [("pF", 256, 1), ("pF", 1, 2), ("pF", 257, 2), ("pF", 1, 2)]
        Go = [("pF", 0), ("pF", 256), ("pF", 0), (GT, gpos)]
        Ts = [("TS", 0, 1), ("TS", 257, 2), ("TS", 513, 2), ("TS", 641, 2)]
        To = [("TS", 256), ("TS", 512), ("TS", 640), (GT, tpos)]
        Ks = [("KT", 0, 1), ("KS", 1, 2), ("KS", 257, 2), ("KS", 385, 2)]
        Ko = [("KS", 0), ("KS", 256), ("KS", 384), ("KS", 448)]
        cpos = (0, 256, 384, 448)

        def prefix_t(h):
            n = cut[h + 1] - cut[h]
            scan(C("TS", cut[h], cut[h + 1]), C("mask", 0, n), C("pB" if h == 0 else "pD", 0, n), ALU.mult, ALU.add)

        def prefix_g(h):
            n = cut[h + 1] - cut[h]
            scan(C("pF", 256 + cut[h], 256 + cut[h + 1]), C("mask", 0, n), C("pC" if h == 0 else "pE", 0, n), ALU.mult, ALU.add)

        def level(lv, h, f1, f2):
            m, at = (cut[h + 1] - cut[h], cut[h]) if lv == 0 else (256 >> lv, 0)

            def view(src, first, step):
                lo = src[1] + at * src[2]
                return C(src[0], lo + first * src[2], lo + (m - 1) * src[2] + 1, src[2] * step)

            def out(dst):
                return C(dst[0], dst[1] + at, dst[1] + at + m)
            c = C("cb", cpos[lv] + at, cpos[lv] + at + m)
            p1 = C("pA", 384, 384 + m // 2)
            tt(p1, view(Gs[lv], 1, 2), view(Ts[lv], 0, 2), ALU.mult)
            tt(C("p2", 0, m // 2), view(Gs[lv], 0, 2), view(Ts[lv], 1, 2), ALU.mult)
            f1()
            tt(C("cb", cpos[lv] + at + 1, cpos[lv] + at + m, 2), p1, C("p2", 0, m // 2), ALU.is_gt)
            f2()
            scan(out(Go[lv]), c, view(Gs[lv], 0, 1), ALU.add, ALU.min)
            scan(out(To[lv]), c, view(Ts[lv], 0, 1), ALU.add, ALU.min)
            if lv == 3:
                send(t, "G", GT)
            scan(out(Ko[lv]), c, view(Ks[lv], 0, 1), ALU.add, ALU.min)

        gaps = [lambda: cp(C("si", 0, 16), C("pC", 256, 272)),
                lambda: ts(C("si", 16, 32), C("si", 0, 16), 15, ALU.bitwise_and),
                lambda: tt(C("sm", 0, 16), C("si", 16, 32), i16, ALU.add),
                lambda: cp(lsC, C("sm", 0, 16)),
                lambda: tt(C("F0", 33, 64, 2), C("sm", 0, 16), dmp if t < 3 else dmp3x, ALU.subtract)]

        def gap():
            if todo:
                max_scan(1)
            elif gaps:
                gaps.pop(0)()
        for j in range(4):
            c0, c1, h = 4 * j, 4 * j + 4, int(64 * j >= H0)
            bt, bg, lo = ("pB", "pD")[h], ("pC", "pE")[h], 64 * j - cut[h]
            x0 = 256 * c0
            for a in range(16):
                mat(C(bt, lo, lo + 64), C("SEL", 15 - a, 143 - a), C("xg", x0 + 64 * a, x0 + 64 * a + 64), False, 64 * j + 64 == cut[h + 1] and a == 15)
            if j < 3:
                for k in range(16):
                    tt(C("mm", x0 + k, x0 + 1024, 16), C("xg", x0 + k, x0 + 1024, 16), C("pA", 16 * c0, 16 * c1), ALU.min)
            else:
                tt(C("mm", x0, x0 + 512), C("xg", x0, x0 + 512), A("pG"), ALU.min)
                prefix_t(0)
                prefix_g(0)
                n0 = len(ops)
                gap()
                level(0, 0, gap, gap if PAR["LB"] > 5 else lambda: None)
                held = ops[n0 + PAR["LB"]:]
                del ops[n0 + PAR["LB"]:]
                tt(C("mm", x0 + 512, x0 + 1024), C("xg", x0 + 512, x0 + 1024), A("pH"), ALU.min)
            for a in range(16):
                mat(C(bg, lo, lo + 64), C("SEL", 15 - a, 143 - a), C("mm", x0 + 64 * a, x0 + 64 * a + 64), a == 0, a == 15)
            if j == PAR["J2"] and PAR["N2"][t]:
                cp(C("xg", 256 * (12 - PAR["N2"][t]), 3072), records(12 - PAR["N2"][t], 12))
            if j < 3:
                for n in range(PAR["S1"][j]):
                    max_scan(1)
                    if n < PAR["G1"][j] and gaps:
                        gaps.pop(0)()
        act(A("zr"), A(zt), ACT.Relu, bias=-1.75)
        early = len(gaps) < 2
        if early:
            act(C("XV", 0, 256), pick(C("X", 0, 4096), lsC), bias=192.0)
        if not sum(PAR["G1"]):
            u_small()
        ops.extend(held[:-1])
        prefix_t(1)
        ops.extend(held[-1:])
        max_scan(PAR["NT"])
        prefix_g(1)
        PZ = ((0, NA, "pG", 0), (NA, 256, "pH", 0))
        for lo, hi, bank, at in PZ:
            mat(C(bank, at + lo, at + hi), HALF, C("zr", lo, hi), True, False)
        if t < 3:
            u_start("pB", 0, 256, True)
            u_start("pE", NA, 256, True)
        else:
            for j, bank in enumerate(("pB", "pE", "pB", "pE")):
                col, at = 512 * j, 512 * j + 128 * (j // 2)
                mat(A(bank), IDN, C("X", col, col + 512), True, False)
                mat(A(bank), SIXT, C("X", 2048 + col, 2560 + col), False, True)
                act(C("YX", at, at + 512), A(bank))
        gap()
        for lv in range(4):
            level(lv, 1 if lv == 0 else 0, gap, gap)
        Kb = C("KS", 449, 480, 2)
        gap()
        ts(lsY, Kb, 4096.0, ALU.mult)
        YS = PAR["YS"]
        if split(t):
            act(C(Y, 0, NA), pick(C("PM", 0, 16 * NA), C("ls", 0, NA // 16)), scale=0.5)
            send(t, "Y", Y)
            max_scan(len(todo) - (16 - YS))
            act(C(Y, NA, 16 * YS), pick(C("PM", 0, 256 * YS), C("ls", NA // 16, YS)), scale=0.5)
            max_scan(16)
        else:
            max_scan(16)
            act(C(Y, 0, 16 * YS), pick(C("PM", 0, 256 * YS), C("ls", 0, YS)), scale=0.5)
        tt(C("sm", 16, 32), Kb, cj, ALU.add)
        ts(C(Y, 16 * YS, 256), pick(A("PM"), C("ls", YS, 16)), 0.5, ALU.mult)
        send(t, "Z" if split(t) else "Y", Y)
        rival_part(t, range(16 - late(t), 16), [A(Y)])

        def splice():
            tab = A("Tab", key="TabA")[1] + A("Tab", key="TabB")[1]
            for h in range(2):
                ts(C("Jw", 128 * h, 128 * h + 128), pick((T.Tab[:], tab), C("ls", 64 + 8 * h, 72 + 8 * h)), 4095 << (12 * h), ALU.bitwise_and)
            for lo, hi, _, at in PARTS:
                cp(C(JJ, at, at + hi - lo), C("Jw", lo, hi))

        def q_win(parts):
            for lo, hi, _, at in parts if t < 3 else ():
                tt(C("Q2", at, at + hi - lo), C("pB", lo, hi), C("Jw", lo, hi), ALU.mult)

        def first_calls():
            ts(lsJ, C("sm", 16, 32), 2.0 ** 19, ALU.mult)
            tt(A("b1"), Kb, kb0, ALU.subtract)
            if JW == 0:
                splice()

        def rest_gaps():
            while gaps:
                gaps.pop(0)()
        JW, QW = PAR["JW"][t], PAR["QW"][t]
        mat(C("pD", 256, 512), IDN, A(zt), True, False)
        mat(C("pD", 256, 512), NEG2, A(Y), False, True)
        act(A("ab"), C("pD", 256, 512), ACT.Abs)
        n0 = len(ops)
        weave(rest_gaps, first_calls)
        behind = ops[n0 + PAR["ZW"]:]
        del ops[n0 + PAR["ZW"]:]
        for lo, hi, _, at in PARTS:
            ts(C("Z2", at, at + hi - lo), C("ab", lo, hi), 1.0, ALU.max, 192.0, ALU.add)
        ops.extend(behind)
        if not early:
            act(C("XV", 0, 256), pick(C("X", 0, 4096), lsC), bias=192.0)
        if t < 3:
            u_start("pD", 0, NA, True)
            for lo, hi, _, at in PARTS:
                mat(C("pF", lo, hi), W2, C("Z2", at, at + hi - lo), True, True)
            for lo, hi, _, at in PARTS:
                u_sum("pB", lo, hi, "Z2", at)
            u_cast("pF", 0, 256, "tw", True)
        mat(C("pC", 256, 512), HALF, C("XV", 0, 256), True, False)
        mat(C("pC", 256, 512), IDN, A(Y), False, True)
        act(C("XV", 256, 512), C("pC", 256, 512), bias=95.75)
        if t < 3:
            u_rest("pB", 0, 256, "tw")
        else:
            cp(C("F1", 33, 64, 2), dmp3)
            tt(C("sm", 64, 80), C("F0", 33, 64, 2), dmp3, ALU.add)
            tt(C("dl", 0, 256), C("XV", 256, 512), C("XV", 0, 256), ALU.subtract)
            cp(C("ls", 80, 96), C("sm", 64, 80))
            ts(C("dl", 256, 384), C("dl", 128, 256), 16.0, ALU.mult)
            for h in range(2):
                tt(C("sv", 64 * h, 64 * h + 64), pick(yx(h), C("ls", 80 + 4 * h, 84 + 4 * h)), C("dl", 64 * h, 64 * h + 64), ALU.add)
        if JW == 1:
            splice()
        if QW == 0:
            q_win(PARTS)
        tt(C("sm", 32, 64), C(GT, 1, 64, 2), C(GP, 1, 64, 2), ALU.mult)
        for j in range(2):
            win = C("F1", 32 * j, 32 * j + 32, 2)
            if lower:
                tt(win, C("sm", 32, 48), C("sm", 48, 64), ALU.is_ge)
            else:
                tt(win, C("sm", 48, 64), C("sm", 32, 48), ALU.is_gt)
        if t < 3:
            tt(A("wb"), C("F1", 0, 32, 2), A("b1"), ALU.mult)
        scan(A("F2"), A("F0"), A("F1"), ALU.mult, ALU.add)
        if QW == 1:
            q_win(PARTS[:1])
        cp(C("ls", 32, 64), C("F2", 1, 64, 2))
        if QW == 1:
            q_win(PARTS[1:])
        if t == 3:
            def low(h):
                cp(pick(yx(h, 128), C("ls", 48 + 4 * h, 52 + 4 * h)), C("sv", 64 * h, 64 * h + 64))

            def high(h):
                tt(C("sv", 128 + 64 * h, 192 + 64 * h), pick(yx(h), C("ls", 88 + 4 * h, 92 + 4 * h)), C("dl", 256 + 64 * h, 320 + 64 * h), ALU.add)
                cp(pick(yx(h, 128), C("ls", 56 + 4 * h, 60 + 4 * h)), C("sv", 128 + 64 * h, 192 + 64 * h))
                dma("Y", C("yx", 1024 * h, 1024 * h + 1024), C("YX", 1152 * h, 1152 * h + 1024), "out%d" % (2 + h))
            low(0)
            low(1)
            high(0)
            high(1)
            if JW == 2:
                splice()

        def names(parts):
            for lo, hi, at, _ in parts:
                act(C("JJ%d" % (t + 1), at, at + hi - lo), pick(A(JJ), C("ls", 32 + lo // 16, 32 + hi // 16)))
        if t < 3:
            mat(C("pA", 256, 272), A("BIG"), A("wb"), True, True)
            act(A("junk"), C("pA", 256, 272), acc=A32)
            JE = PAR["JE"][t]
            names(PARTS[:JE])

        def names_store():
            act(C("Jo", 0, 128), pick(A(JJ), C("ls", 32, 40)))
            act(C("Jo", 128, 256), pick(A(JJ), C("ls", 40, 48)), scale=2.0 ** -12)
            dma("S", A("yj"), A("Jo"), "out1")
        if t == 3 and JW < 2:
            names_store()

        def z_lose(part):
            (lo, hi, bank, at), to = PZ[part], PARTS[part][2]
            mat(C(bank, at + lo, at + hi), IDN, C("YP%d" % t, lo, hi), False, True)
            act(C("Z2", to, to + hi - lo), C(bank, at + lo, at + hi), bias=192.4375)
        z_lose(0)
        z_lose(1)
        if t < 3:
            if PAR["JM"][t]:
                factors("Z2", (0, 2 * NA), (0,))
                names(PARTS[JE:])
                factors("Z2", (0, 2 * NA), (1,))
            else:
                factors("Z2", (0, 2 * NA), (0, 1))
                names(PARTS[JE:])
        act(A("z%d" % (t + 1)), pick(A("Z2"), lsW), bias=-192.0)
        if t < 3:
            tt(pick(A("X"), lsX), C("XV", 256, 512), A("m192"), ALU.add)
            if QW == 2:
                q_win(PARTS)
            both_lists(t + 1, t)
    dma("S", A("yz"), A("z4"), "out4")
    if JW == 2:
        names_store()
    emit(g, T, ops, left[0])


def rank_program(g, core, T, topo):
    rank = T.rank_of(core)
    if rank is None:
        relay_program(g, core, T, topo)
    else:
        build_rank(g, core, T, topo, rank)
